import numpy as np
import ml_dtypes


def mxq(x, axis, fmt="e4m3"):
    dtype, down = {"e4m3": (ml_dtypes.float8_e4m3fn, 7), "e5m2": (ml_dtypes.float8_e5m2, 14)}[fmt]
    v = np.moveaxis(np.asarray(x, np.float32).astype(ml_dtypes.bfloat16).astype(np.float64), axis, -1)
    blocks = v.reshape(v.shape[:-1] + (-1, 32))
    amax = np.abs(blocks).max(-1, keepdims=True)
    byte = np.maximum(np.where(amax > 0, np.frexp(amax)[1] - 1 + 127, 0) - down, 1)
    scale = np.exp2(byte - 127.0)
    codes = (blocks / scale).astype(np.float32).astype(dtype).astype(np.float64)
    return np.moveaxis((codes * scale).reshape(v.shape), -1, axis)


WIDE = False


def mx_kscale(k):
    if not WIDE:
        return np.ones(k)
    levels = np.array([10, -10, 5, -5, 0])
    if k % 512:
        return np.exp2(np.random.permutation(np.resize(levels, k // 32))).repeat(32)
    a = np.empty((k // 512, 16))
    for p in range(k // 512):
        a[p, :8] = np.random.permutation(np.resize(levels, 8))
        for g in range(8):
            far = levels[np.abs(levels - a[p, g]) >= 10]
            a[p, g + 8] = far[np.random.randint(len(far))]
    return np.exp2(a.ravel()).repeat(32)


BF16 = ml_dtypes.bfloat16


def bf(x):
    return np.asarray(x, np.float32).astype(BF16)


def f64(x):
    return np.asarray(x).astype(np.float64)


E2M1 = np.array([0.0, 0.5, 1.0, 1.5, 2.0, 3.0, 4.0, 6.0, -0.0, -0.5, -1.0, -1.5, -2.0, -3.0, -4.0, -6.0])


def pack_weight(w, fmt):
    k, n = w.shape
    w = f64(bf(w)).reshape(k // 32, 32, n)
    amax = np.abs(w).max(1)
    if fmt == "e4m3":
        byte = np.frexp(amax)[1] - 1 + 127 - 7
    else:
        mant, ex = np.frexp(amax / 6.0)
        byte = np.where(mant > 0.5, ex, ex - 1) + 127
    byte = np.clip(np.where(amax > 0, byte, 1), 1, 254)
    scaled = (w * np.exp2(127.0 - byte)[:, None, :]).reshape(k, n).astype(np.float32)
    by_word = np.ascontiguousarray(scaled.reshape(k // 512, 128, 4, n).transpose(0, 1, 3, 2))
    if fmt == "e4m3":
        words = by_word.astype(ml_dtypes.float8_e4m3fn).view(np.uint8)
    else:
        c = by_word.astype(ml_dtypes.float4_e2m1fn).view(np.uint8) & 0xF
        words = c[..., 0::2] | (c[..., 1::2] << 4)
    return np.ascontiguousarray(words), np.ascontiguousarray(byte.astype(np.uint8).reshape(k // 512, 16, n))


def unpack_weight(words, scales, fmt):
    g, p, n, _ = words.shape
    if fmt == "e4m3":
        vals = np.ascontiguousarray(words).view(ml_dtypes.float8_e4m3fn).astype(np.float64)
    else:
        nib = np.empty((g, p, n, 4), np.uint8)
        nib[..., 0::2] = words & 0xF
        nib[..., 1::2] = words >> 4
        vals = E2M1[nib]
    vals = vals * np.repeat(np.exp2(scales.astype(np.float64) - 127.0), 8, axis=1)[..., None]
    return vals.transpose(0, 1, 3, 2).reshape(g * 512, n)
def pack4(w):
    words, scales = pack_weight(w, "e2m1")
    return words.reshape(words.shape[0], 128, -1), scales


def unpack4(words, scales):
    return unpack_weight(words.reshape(words.shape[0], 128, -1, 2), scales, "e2m1")


H, D, T, M, N = 8, 128, 2048, 512, 2048


def setup_inputs():
    s, t = mx_kscale(T), mx_kscale(H * D)
    e = np.exp(1.5 * np.random.standard_normal((H, T, M)))
    probs = e / e.sum(axis=1, keepdims=True)
    tok_scale = np.sqrt(T) / 4 * np.exp(0.3 * np.random.standard_normal((H, T)))
    v = np.random.standard_normal((T, H * D)) / s[:, None] * t
    wo = np.random.standard_normal((H * D, N)) / np.sqrt(H * D) / t[:, None]
    v_words, v_scales = pack4(v)
    wo_words, wo_scales = pack4(wo)
    return {"probs": bf(probs),
            "tok_scale": bf(tok_scale * s),
            "v_words": v_words,
            "v_scales": v_scales,
            "v_bias": bf(0.3 * np.random.standard_normal(H * D) * t),
            "wo_words": wo_words,
            "wo_scales": wo_scales}


def reference(probs, tok_scale, v_words, v_scales, v_bias, wo_words, wo_scales):
    a = f64(probs) * f64(tok_scale)[:, :, None]
    aq = mxq(a, 1, "e4m3")
    v = unpack4(v_words, v_scales).reshape(T, H, D).transpose(1, 2, 0)
    o = v @ aq
    o = o.reshape(H * D, M) + f64(v_bias)[:, None]
    out = mxq(o, 0, "e4m3").T @ unpack4(wo_words, wo_scales)
    return out

@@ -1,0 +1,385 @@
+from contextlib import ExitStack
+
+import concourse.mybir as mybir
+from concourse.masks import make_identity
+
+H, D, T, M, N = 8, 128, 2048, 512, 2048
+FLOPS = 2 * H * D * T * M + 2 * M * H * D * N
+
+F32 = mybir.dt.float32
+BF16 = mybir.dt.bfloat16
+I32 = mybir.dt.int32
+U32 = mybir.dt.uint32
+U8 = mybir.dt.uint8
+FP8X4 = mybir.dt.float8_e4m3fn_x4
+FP4X4 = mybir.dt.float4_e2m1fn_x4
+MULT = mybir.AluOpType.mult
+ADD = mybir.AluOpType.add
+
+P = 128
+PACK = 4
+K_PASS = P * PACK
+G = T // K_PASS
+QT = M // P
+G2 = H * D // K_PASS
+HEADS_PER_PASS = K_PASS // D
+R_TILE = 512
+RT = N // R_TILE
+UNITS = H * G
+LATE_HEADS = 2
+EARLY_HEADS = H - LATE_HEADS
+LATE = EARLY_HEADS * G
+RUN = 4
+SKEW = 1
+LATE_ORDER = sorted(((q, j) for q in range(QT) for j in range(LATE_HEADS)), key=lambda e: (LATE_HEADS * e[0] + SKEW * e[1], e[0]))
+
+RAW_BUFS = 14
+SCALAR_SHARE = 0.83
+LATE_SHARE = 0.7
+END_SHARE = 0.3
+END_FROM = 29
+EXTRA_EVERY = 3
+EXTRA_FROM = 8
+EXTRA_NUM = 1
+OUT_BANKS = 6
+OPEN_FROM = 23
+OPEN_AGAIN = 33
+E_STEP = 0
+E_PHASE = 3
+C_STEP = 1
+C_PHASE = 1
+Q_STEP = 1
+Q_PHASE = 3
+P_SPLIT = 2
+P_STEP = 2
+P_PHASE = 2
+O_PHASE = 4
+RES_SPLIT = 12
+P_LAG = 0
+C_FIRST = 0
+X_DELAY = 1
+X_SPLIT = 2
+X_PHASE = 4
+VECTOR_OUT_FROM = 8
+FIRST_PRODUCT_STEP = 9
+
+
+def tile_fp4_value_cache_projection_s13_kernel(
+    tc, probs, tok_scale, v_words, v_scales, v_bias, wo_words, wo_scales, out
+):
+    nc = tc.nc
+    with ExitStack() as ctx:
+        keep = ctx.enter_context(tc.tile_pool(name="keep", bufs=1))
+        raw_pool = ctx.enter_context(tc.tile_pool(name="raw", bufs=RAW_BUFS))
+        grp_pool = ctx.enter_context(tc.tile_pool(name="grp", bufs=4))
+        code_pool = ctx.enter_context(tc.tile_pool(name="code", bufs=10))
+        small_pool = ctx.enter_context(tc.tile_pool(name="small", bufs=2))
+        res_pool = ctx.enter_context(tc.tile_pool(name="res", bufs=4))
+        head_psum = ctx.enter_context(tc.psum_pool(name="head_psum", bufs=1))
+        turn_psum = ctx.enter_context(tc.psum_pool(name="turn_psum", bufs=1))
+        out_psum = ctx.enter_context(tc.psum_pool(name="out_psum", bufs=OUT_BANKS))
+        ctx.enter_context(tc.manual_schedule())
+
+        ident = keep.tile([P, P], F32)
+        v_code = keep.tile([P, G, 2 * H * D], U8, align_bytes=64)
+        v_plane = keep.tile([P, G, H * D], U8, align_bytes=64)
+        w_code = keep.tile([P, G2, 2 * N], U8, align_bytes=64)
+        w_plane = keep.tile([P, G2, N], U8, align_bytes=64)
+        bias = keep.tile([P, H * D], BF16)
+        late_raw = [keep.tile([P, G, PACK, M], BF16, name="late_raw%d" % j) for j in range(LATE_HEADS)]
+        factors = [keep.tile([P, G, PACK], BF16, name="factor%d" % h) for h in range(H)]
+        o_rows = [keep.tile([P, QT, K_PASS], BF16, name="o_rows%d" % g) for g in range(G2)]
+        o_first = keep.tile([P, M * PACK], BF16, align_bytes=64)
+        o_first_code = keep.tile([P, M], U32, align_bytes=64)
+        o_first_plane = keep.tile([P, M], U8, align_bytes=64)
+
+        raw = {}
+        grouped = {}
+        a_code = {}
+        a_plane = {}
+        head_sum = {}
+        late_sum = {}
+        turned = {}
+        o_last = {}
+        o_last_code = {}
+        o_last_plane = {}
+        out_sum = {}
+        staged = {}
+
+        def load_factor(h, queue):
+            queue.dma_start(out=factors[h][:], in_=tok_scale[h].rearrange("(g p t) -> p g t", p=P, t=PACK))
+
+        def load_words(dst, src, g0, g1):
+            nc.sync.dma_start(
+                out=dst[:, g0:g1, :].bitcast(I32), in_=src[g0:g1].rearrange("g p n -> p g n").bitcast(I32)
+            )
+
+        def load_plane(dst, src):
+            for r in range(4):
+                nc.sync.dma_start(
+                    out=dst[r:P:32, :, :].bitcast(I32),
+                    in_=src[:, r:16:4, :].rearrange("g q n -> q g n").bitcast(I32),
+                )
+
+        def load_raw(i):
+            h, g = divmod(i, G)
+            if g == 0 and h > 0:
+                load_factor(h, nc.sync)
+            if i < LATE:
+                raw_tile = raw_pool.tile([P, PACK, M], BF16)
+                raw[i] = raw_tile[:]
+            else:
+                raw[i] = late_raw[h - EARLY_HEADS][:, g, :, :]
+            rows = probs[h, g * K_PASS : (g + 1) * K_PASS, :]
+            nc.sync.dma_start(out=raw[i], in_=rows.rearrange("(p t) i -> p t i", t=PACK))
+            if i == 3:
+                load_words(v_code, v_words, 0, 2)
+            if i == 5:
+                load_words(v_code, v_words, 2, 4)
+            if i == 6:
+                load_plane(v_plane, v_scales)
+            if i == 8:
+                nc.sync.dma_start(out=bias[:], in_=v_bias.partition_broadcast(P))
+            if i == UNITS - 1:
+                load_plane(w_plane, wo_scales)
+                load_words(w_code, wo_words, 0, 1)
+                load_words(w_code, wo_words, 1, 2)
+
+        def scale_rows(i):
+            h, g = divmod(i, G)
+            for t in range(PACK):
+                row = raw[i][:, t, :]
+                nc.vector.tensor_scalar(
+                    out=row, in0=row, scalar1=factors[h][:, g, t : t + 1], scalar2=None, op0=MULT
+                )
+
+        def interleave(u):
+            assert state['scaled'] > (u if u < LATE else LATE + G * LATE_ORDER[u - LATE][1] + 3), u
+            grp = grp_pool.tile([P, M * PACK], BF16, align_bytes=64)
+            grouped[u] = grp
+            if u < LATE:
+                src = raw[u].rearrange("p t (c i) -> p c t i", i=RUN)
+                dst = grp[:].rearrange("p (c i t) -> p c t i", i=RUN, t=PACK)
+                runs = M // RUN
+                cut = int(runs * SCALAR_SHARE) // 2 * 2
+                nc.scalar.copy(out=dst[:, :cut], in_=src[:, :cut])
+                nc.vector.tensor_copy(out=dst[:, cut:], in_=src[:, cut:])
+            else:
+                q, j = LATE_ORDER[u - LATE]
+                src = late_raw[j][:, :, :, q * P : (q + 1) * P].rearrange("p g t (c i) -> p g c t i", i=RUN)
+                dst = grp[:].rearrange("p (g c i t) -> p g c t i", g=G, i=RUN, t=PACK)
+                runs = P // RUN
+                cut = int(runs * (LATE_SHARE if u < END_FROM else END_SHARE)) // 2 * 2
+                if cut > 0:
+                    nc.scalar.copy(out=dst[:, :, :cut], in_=src[:, :, :cut])
+                nc.vector.tensor_copy(out=dst[:, :, cut:], in_=src[:, :, cut:])
+
+        def quantise(u):
+            code = code_pool.tile([P, M], U32, align_bytes=64)
+            plane = code_pool.tile([P, M], U8, align_bytes=64)
+            a_code[u] = code
+            a_plane[u] = plane
+            nc.vector.quantize_mx(out=code[:].bitcast(FP8X4), scales=plane[:], in_=grouped[u][:])
+
+        def value_pass(dst, u, block, h, g):
+            cols = slice(block * P, (block + 1) * P)
+            nc.tensor.matmul_mx(
+                out=dst,
+                lhsT=a_code[u][:, cols].bitcast(FP8X4),
+                lhsT_scale=a_plane[u][:, cols],
+                rhs=v_code[:, g, 2 * h * D : 2 * (h + 1) * D].bitcast(FP4X4),
+                rhs_scale=v_plane[:, g, h * D : (h + 1) * D],
+                start=(g == 0),
+                stop=(g == G - 1),
+            )
+
+        def head_product(h):
+            acc = head_psum.tile([P, QT, D], F32, tag="head")
+            head_sum[h] = acc
+            for q in range(QT):
+                for g in range(G):
+                    value_pass(acc[:, q, :], h * G + g, q, h, g)
+
+        def head_add_bias(h):
+            g2, j = divmod(h, HEADS_PER_PASS)
+            nc.vector.tensor_tensor(
+                out=o_rows[g2][:, :, j * D : (j + 1) * D],
+                in0=head_sum[h][:],
+                in1=bias[:, h * D : (h + 1) * D].unsqueeze(1).to_broadcast([P, QT, D]),
+                op=ADD,
+            )
+
+        def late_product(u):
+            q, j = LATE_ORDER[u - LATE]
+            if j == 0:
+                acc = head_psum.tile([P, QT, D], F32, tag="head")
+                late_sum[q] = acc
+            for g in range(G):
+                value_pass(late_sum[q][:, j, :], u, g, EARLY_HEADS + j, g)
+
+        def late_add_bias(q):
+            nc.vector.tensor_tensor(
+                out=o_rows[G2 - 1][:, q, K_PASS - LATE_HEADS * D :],
+                in0=late_sum[q][:, :LATE_HEADS, :].rearrange("p j d -> p (j d)"),
+                in1=bias[:, EARLY_HEADS * D :],
+                op=ADD,
+            )
+
+        def turn(dst, g2, q):
+            words = o_rows[g2][:, q, :].bitcast(F32)
+            for u in range(2):
+                nc.tensor.transpose(dst[:, u, :], words[:, u : 2 * P : 2], ident[:])
+
+        def first_turn(half):
+            bank = turn_psum.tile([P, 2, 2, P], F32, tag="turn")
+            for j in range(2):
+                turn(bank[:, j], 0, 2 * half + j)
+            dst = o_first[:, half * 2 * K_PASS : (half + 1) * 2 * K_PASS].bitcast(F32)
+            nc.scalar.copy(
+                out=dst.rearrange("p (j q u) -> p j q u", j=2, u=2),
+                in_=bank[:].rearrange("p j u q -> p j q u"),
+            )
+
+        def first_quantise():
+            nc.vector.quantize_mx(out=o_first_code[:].bitcast(FP8X4), scales=o_first_plane[:], in_=o_first[:])
+
+        def late_turn(q):
+            bank = turn_psum.tile([P, 2, 2, P], F32, tag="turn")
+            turned[q] = bank
+            turn(bank[:, 0], G2 - 1, q)
+
+        def late_copy(q):
+            o_tile = small_pool.tile([P, K_PASS], BF16, align_bytes=64)
+            o_last[q] = o_tile
+            nc.scalar.copy(
+                out=o_tile[:].bitcast(F32).rearrange("p (q u) -> p q u", u=2),
+                in_=turned[q][:, 0].rearrange("p u q -> p q u"),
+            )
+
+        def late_quantise(q):
+            o_code = small_pool.tile([P, P], U32, align_bytes=64)
+            o_plane = small_pool.tile([P, P], U8, align_bytes=64)
+            o_last_code[q] = o_code
+            o_last_plane[q] = o_plane
+            nc.vector.quantize_mx(out=o_code[:].bitcast(FP8X4), scales=o_plane[:], in_=o_last[q][:])
+
+        def project(q, r, g2):
+            if g2 == 0:
+                acc = out_psum.tile([P, R_TILE], F32, tag="out")
+                out_sum[q, r] = acc
+                code = o_first_code[:, q * P : (q + 1) * P]
+                plane = o_first_plane[:, q * P : (q + 1) * P]
+            else:
+                code = o_last_code[q][:]
+                plane = o_last_plane[q][:]
+            nc.tensor.matmul_mx(
+                out=out_sum[q, r][:],
+                lhsT=code.bitcast(FP8X4),
+                lhsT_scale=plane,
+                rhs=w_code[:, g2, 2 * r * R_TILE : 2 * (r + 1) * R_TILE].bitcast(FP4X4),
+                rhs_scale=w_plane[:, g2, r * R_TILE : (r + 1) * R_TILE],
+                start=(g2 == 0),
+                stop=(g2 == G2 - 1),
+            )
+
+        def store(q, r):
+            pair, j = divmod(r, 2)
+            if j == 0:
+                res = res_pool.tile([P, 2, R_TILE], F32)
+                staged[q, pair] = res
+            dst = staged[q, pair][:, j, :]
+            if q * RT + r >= VECTOR_OUT_FROM and r % 2 == 1:
+                nc.vector.tensor_copy(out=dst, in_=out_sum[q, r][:])
+            else:
+                nc.scalar.copy(out=dst, in_=out_sum[q, r][:])
+            if q * RT + r >= RES_SPLIT:
+                nc.sync.dma_start(out=out[q * P : (q + 1) * P, r * R_TILE : (r + 1) * R_TILE], in_=dst)
+            elif j == 1:
+                nc.sync.dma_start(
+                    out=out[q * P : (q + 1) * P, pair * 2 * R_TILE : (pair + 1) * 2 * R_TILE],
+                    in_=staged[q, pair][:].rearrange("p j n -> p (j n)"),
+                )
+
+        load_factor(0, nc.scalar)
+        nc.vector.memset(v_plane[:].bitcast(U32), 0)
+        nc.vector.memset(w_plane[:].bitcast(U32), 0)
+        make_identity(nc, ident[:])
+        for i in range(RAW_BUFS):
+            load_raw(i)
+        loaded = RAW_BUFS
+
+        product_step = {max(G * h + G, FIRST_PRODUCT_STEP + 2 * h): h for h in range(EARLY_HEADS)}
+        first_pass_ready = max(s for s, h in product_step.items() if h == HEADS_PER_PASS - 1) + 1
+        closing_step = {LATE + LATE_ORDER.index((q, LATE_HEADS - 1)) + 1: q for q in range(QT)}
+        closes = sorted(closing_step)
+
+        plan = {}
+
+        def at(step, phase, job, *args):
+            plan.setdefault((step, phase), []).append((job, args))
+
+        state = {"opened": 0, "stored": 0, "scaled": 1}
+
+        def open_banks():
+            while state["opened"] < min(QT * RT, state["stored"] + OUT_BANKS):
+                project(*divmod(state["opened"], RT), 0)
+                state["opened"] = state["opened"] + 1
+
+        def close_bank(q, r):
+            while state["opened"] <= q * RT + r:
+                project(*divmod(state["opened"], RT), 0)
+                state["opened"] = state["opened"] + 1
+            project(q, r, 1)
+
+        def empty_bank(q, r):
+            store(q, r)
+            state["stored"] = state["stored"] + 1
+
+        for u in range(UNITS):
+            at(u + 1, 0, quantise, u)
+            if u >= 1:
+                at(u - 1, 2, interleave, u)
+            if u >= LATE:
+                q = LATE_ORDER[u - LATE][0]
+                free = closes[q - 1] if q > 0 else LATE + 1
+                if u + 1 > free:
+                    at(u + 1, 1, late_product, u)
+                else:
+                    at(free, 4, late_product, u)
+        for step, h in product_step.items():
+            at(step, 1, head_product, h)
+            at(step + 1, 0, head_add_bias, h) if h < EARLY_HEADS - 1 else at(step + 1, 3, head_add_bias, h)
+        at(first_pass_ready + 1, 3, first_turn, 0)
+        at(first_pass_ready + 2, 3, first_turn, 1)
+        at(first_pass_ready + 4, 3, first_quantise)
+        at(OPEN_FROM, 5, open_banks)
+        for step, q in closing_step.items():
+            at(step, 3, late_add_bias, q)
+            at(step, 3, late_turn, q)
+        for step, q in closing_step.items():
+            at(step + 2, 1, late_quantise, q)
+            for r in range(RT):
+                at(step + 2 + (P_LAG if r >= 2 and q < QT - 2 else 0), 1 if r < 2 else 3, close_bank, q, r)
+                at(step + 2 + r // 2, 4 if r < 2 else X_PHASE, empty_bank, q, r)
+        for s in range(OPEN_FROM + 1, UNITS + 3):
+            at(s, 3, open_banks)
+        for step, q in closing_step.items():
+            at(step, 4, late_copy, q)
+
+        scale_rows(0)
+        interleave(0)
+        scale_rows(1)
+        scaled = 2
+        state['scaled'] = 2
+        for s in range(UNITS + 6):
+            for phase in range(6):
+                for job, args in plan.get((s, phase), []):
+                    job(*args)
+            ahead = min(UNITS, s + 3 + max(0, (s - EXTRA_FROM) * EXTRA_NUM // EXTRA_EVERY + 1))
+            while loaded < min(UNITS, s + 2 + RAW_BUFS):
+                load_raw(loaded)
+                loaded = loaded + 1
+            while scaled < ahead:
+                scale_rows(scaled)
+                scaled = scaled + 1
+                state['scaled'] = scaled

@@ -26,21 +26,28 @@ HEADS_PER_PASS = K_PASS // D
 R_TILE = 512
 RT = N // R_TILE
 UNITS = H * G
-LATE_HEADS = 2
+LATE_HEADS = 3
 EARLY_HEADS = H - LATE_HEADS
 LATE = EARLY_HEADS * G
 RUN = 4
 SKEW = 1
 LATE_ORDER = sorted(((q, j) for q in range(QT) for j in range(LATE_HEADS)), key=lambda e: (LATE_HEADS * e[0] + SKEW * e[1], e[0]))
 
-RAW_BUFS = 14
-SCALAR_SHARE = 0.83
+RAW_BUFS = 6
+SINGLE_LOADS = 2
+V_AT = 3
+BIAS_STEP = 4
+OPEN_RATE = 2
+SCALAR_SHARE = 0.82
+EARLY_SHARE = 0.64
+EARLY_TO = 9
+CODE_BUFS = 13
 LATE_SHARE = 0.7
-END_SHARE = 0.3
-END_FROM = 29
-EXTRA_EVERY = 3
-EXTRA_FROM = 8
-EXTRA_NUM = 1
+END_SHARE = 0.35
+END_FROM = 24
+EXTRA_EVERY = 4
+EXTRA_FROM = 9
+EXTRA_NUM = 3
 OUT_BANKS = 6
 OPEN_FROM = 23
 OPEN_AGAIN = 33
@@ -61,7 +68,7 @@ X_DELAY = 1
 X_SPLIT = 2
 X_PHASE = 4
 VECTOR_OUT_FROM = 8
-FIRST_PRODUCT_STEP = 9
+FIRST_PRODUCT_STEP = 11
 
 
 def tile_fp4_value_cache_projection_s13_kernel(
@@ -72,7 +79,7 @@ def tile_fp4_value_cache_projection_s13_kernel(
         keep = ctx.enter_context(tc.tile_pool(name="keep", bufs=1))
         raw_pool = ctx.enter_context(tc.tile_pool(name="raw", bufs=RAW_BUFS))
         grp_pool = ctx.enter_context(tc.tile_pool(name="grp", bufs=4))
-        code_pool = ctx.enter_context(tc.tile_pool(name="code", bufs=10))
+        code_pool = ctx.enter_context(tc.tile_pool(name="code", bufs=CODE_BUFS))
         small_pool = ctx.enter_context(tc.tile_pool(name="small", bufs=2))
         res_pool = ctx.enter_context(tc.tile_pool(name="res", bufs=4))
         head_psum = ctx.enter_context(tc.psum_pool(name="head_psum", bufs=1))
@@ -86,8 +93,10 @@ def tile_fp4_value_cache_projection_s13_kernel(
         w_code = keep.tile([P, G2, 2 * N], U8, align_bytes=64)
         w_plane = keep.tile([P, G2, N], U8, align_bytes=64)
         bias = keep.tile([P, H * D], BF16)
+        bias_col = keep.tile([P, H * D // P], BF16)
+        tok_rows = keep.tile([P, K_PASS], BF16)
+        factor = keep.tile([P, UNITS, PACK], BF16)
         late_raw = [keep.tile([P, G, PACK, M], BF16, name="late_raw%d" % j) for j in range(LATE_HEADS)]
-        factors = [keep.tile([P, G, PACK], BF16, name="factor%d" % h) for h in range(H)]
         o_rows = [keep.tile([P, QT, K_PASS], BF16, name="o_rows%d" % g) for g in range(G2)]
         o_first = keep.tile([P, M * PACK], BF16, align_bytes=64)
         o_first_code = keep.tile([P, M], U32, align_bytes=64)
@@ -106,8 +115,22 @@ def tile_fp4_value_cache_projection_s13_kernel(
         out_sum = {}
         staged = {}
 
-        def load_factor(h, queue):
-            queue.dma_start(out=factors[h][:], in_=tok_scale[h].rearrange("(g p t) -> p g t", p=P, t=PACK))
+        def spread_factor():
+            bank = turn_psum.tile([P, 2, 2, P], F32, tag="turn")
+            words = tok_rows[:].bitcast(F32)
+            for u in range(2):
+                nc.tensor.transpose(bank[:, 0, u, :], words[:, u : 2 * P : 2], ident[:])
+            nc.scalar.copy(out=factor[:].bitcast(F32), in_=bank[:, 0, :, :UNITS].rearrange("p u k -> p k u"))
+
+        def spread_bias():
+            bank = turn_psum.tile([P, 2, 2, P], F32, tag="turn")
+            cols = bank[:].rearrange("p a b n -> p (a b) n")
+            words = bias_col[:].bitcast(F32)
+            for c in range(4):
+                nc.tensor.transpose(cols[:, c, :], words[:, c : c + 1].to_broadcast([P, P]), ident[:])
+            nc.scalar.copy(
+                out=bias[:].bitcast(F32).rearrange("p (n c) -> p n c", c=4), in_=cols.rearrange("p c n -> p n c")
+            )
 
         def load_words(dst, src, g0, g1):
             nc.sync.dma_start(
@@ -121,36 +144,40 @@ def tile_fp4_value_cache_projection_s13_kernel(
                     in_=src[:, r:16:4, :].rearrange("g q n -> q g n").bitcast(I32),
                 )
 
-        def load_raw(i):
-            h, g = divmod(i, G)
-            if g == 0 and h > 0:
-                load_factor(h, nc.sync)
-            if i < LATE:
-                raw_tile = raw_pool.tile([P, PACK, M], BF16)
-                raw[i] = raw_tile[:]
+        def load_raw(k):
+            h, g = divmod(2 * k, G)
+            if 2 * k < LATE:
+                raw_tile = raw_pool.tile([P, 2, PACK, M], BF16)
+                pair = raw_tile[:]
             else:
-                raw[i] = late_raw[h - EARLY_HEADS][:, g, :, :]
-            rows = probs[h, g * K_PASS : (g + 1) * K_PASS, :]
-            nc.sync.dma_start(out=raw[i], in_=rows.rearrange("(p t) i -> p t i", t=PACK))
-            if i == 3:
+                pair = late_raw[h - EARLY_HEADS][:, g : g + 2]
+            raw[2 * k] = pair[:, 0]
+            raw[2 * k + 1] = pair[:, 1]
+            rows = probs[h, g * K_PASS : (g + 2) * K_PASS, :].rearrange("(g p t) i -> p g t i", p=P, t=PACK)
+            if k < SINGLE_LOADS:
+                for j in range(2):
+                    if k == 0 and j == 0:
+                        nc.sync.dma_start(out=pair[:, j, :2], in_=rows[:, j, :2])
+                        nc.sync.dma_start(out=pair[:, j, 2:], in_=rows[:, j, 2:])
+                    else:
+                        nc.sync.dma_start(out=pair[:, j], in_=rows[:, j])
+            else:
+                nc.sync.dma_start(out=pair, in_=rows)
+            if k == V_AT:
                 load_words(v_code, v_words, 0, 2)
-            if i == 5:
+            if k == V_AT + 1:
                 load_words(v_code, v_words, 2, 4)
-            if i == 6:
                 load_plane(v_plane, v_scales)
-            if i == 8:
-                nc.sync.dma_start(out=bias[:], in_=v_bias.partition_broadcast(P))
-            if i == UNITS - 1:
+            if k == UNITS // 2 - 1:
                 load_plane(w_plane, wo_scales)
                 load_words(w_code, wo_words, 0, 1)
                 load_words(w_code, wo_words, 1, 2)
 
         def scale_rows(i):
-            h, g = divmod(i, G)
             for t in range(PACK):
                 row = raw[i][:, t, :]
                 nc.vector.tensor_scalar(
-                    out=row, in0=row, scalar1=factors[h][:, g, t : t + 1], scalar2=None, op0=MULT
+                    out=row, in0=row, scalar1=factor[:, i, t : t + 1], scalar2=None, op0=MULT
                 )
 
         def interleave(u):
@@ -161,7 +188,7 @@ def tile_fp4_value_cache_projection_s13_kernel(
                 src = raw[u].rearrange("p t (c i) -> p c t i", i=RUN)
                 dst = grp[:].rearrange("p (c i t) -> p c t i", i=RUN, t=PACK)
                 runs = M // RUN
-                cut = int(runs * SCALAR_SHARE) // 2 * 2
+                cut = int(runs * (SCALAR_SHARE if u >= EARLY_TO else EARLY_SHARE)) // 2 * 2
                 nc.scalar.copy(out=dst[:, :cut], in_=src[:, :cut])
                 nc.vector.tensor_copy(out=dst[:, cut:], in_=src[:, cut:])
             else:
@@ -300,13 +327,17 @@ def tile_fp4_value_cache_projection_s13_kernel(
                     in_=staged[q, pair][:].rearrange("p j n -> p (j n)"),
                 )
 
-        load_factor(0, nc.scalar)
+        nc.gpsimd.memset(tok_rows[32:64, :], 0.0)
+        nc.gpsimd.memset(tok_rows[64:, :], 0.0)
+        nc.scalar.dma_start(out=tok_rows[:UNITS, :], in_=tok_scale.rearrange("h (g k) -> (h g) k", g=G))
+        nc.scalar.dma_start(out=bias_col[:], in_=v_bias.rearrange("(p c) -> p c", p=P))
+        make_identity(nc, ident[:])
         nc.vector.memset(v_plane[:].bitcast(U32), 0)
         nc.vector.memset(w_plane[:].bitcast(U32), 0)
-        make_identity(nc, ident[:])
-        for i in range(RAW_BUFS):
-            load_raw(i)
+        for k in range(RAW_BUFS):
+            load_raw(k)
         loaded = RAW_BUFS
+        spread_factor()
 
         product_step = {max(G * h + G, FIRST_PRODUCT_STEP + 2 * h): h for h in range(EARLY_HEADS)}
         first_pass_ready = max(s for s, h in product_step.items() if h == HEADS_PER_PASS - 1) + 1
@@ -320,8 +351,8 @@ def tile_fp4_value_cache_projection_s13_kernel(
 
         state = {"opened": 0, "stored": 0, "scaled": 1}
 
-        def open_banks():
-            while state["opened"] < min(QT * RT, state["stored"] + OUT_BANKS):
+        def open_banks(limit):
+            while state["opened"] < min(limit, state["stored"] + OUT_BANKS):
                 project(*divmod(state["opened"], RT), 0)
                 state["opened"] = state["opened"] + 1
 
@@ -352,19 +383,20 @@ def tile_fp4_value_cache_projection_s13_kernel(
         at(first_pass_ready + 1, 3, first_turn, 0)
         at(first_pass_ready + 2, 3, first_turn, 1)
         at(first_pass_ready + 4, 3, first_quantise)
-        at(OPEN_FROM, 5, open_banks)
+        at(BIAS_STEP, 3, spread_bias)
         for step, q in closing_step.items():
             at(step, 3, late_add_bias, q)
             at(step, 3, late_turn, q)
-        for step, q in closing_step.items():
-            at(step + 2, 1, late_quantise, q)
+            at(step, 5, late_copy, q)
+            at(step + 1, 3, late_quantise, q)
             for r in range(RT):
-                at(step + 2 + (P_LAG if r >= 2 and q < QT - 2 else 0), 1 if r < 2 else 3, close_bank, q, r)
-                at(step + 2 + r // 2, 4 if r < 2 else X_PHASE, empty_bank, q, r)
-        for s in range(OPEN_FROM + 1, UNITS + 3):
-            at(s, 3, open_banks)
-        for step, q in closing_step.items():
-            at(step, 4, late_copy, q)
+                at(step + 1, 3, close_bank, q, r)
+                if q == QT - 2:
+                    at(closes[-1], 2 if r < 3 else 4, empty_bank, q, r)
+                else:
+                    at(step + 2, X_PHASE, empty_bank, q, r)
+        for s in range(OPEN_FROM, UNITS + 1):
+            at(s, 4 if s == closes[-1] else 3, open_banks, OPEN_RATE * (s - OPEN_FROM + 1) if s < closes[0] else QT * RT)
 
         scale_rows(0)
         interleave(0)
@@ -376,7 +408,7 @@ def tile_fp4_value_cache_projection_s13_kernel(
                 for job, args in plan.get((s, phase), []):
                     job(*args)
             ahead = min(UNITS, s + 3 + max(0, (s - EXTRA_FROM) * EXTRA_NUM // EXTRA_EVERY + 1))
-            while loaded < min(UNITS, s + 2 + RAW_BUFS):
+            while loaded < min(UNITS // 2, (s + 2) // 2 + RAW_BUFS):
                 load_raw(loaded)
                 loaded = loaded + 1
             while scaled < ahead:

@@ -33,28 +33,37 @@ RUN = 4
 SKEW = 1
 LATE_ORDER = sorted(((q, j) for q in range(QT) for j in range(LATE_HEADS)), key=lambda e: (LATE_HEADS * e[0] + SKEW * e[1], e[0]))
 
+PAIR_FROM = 20
+E_LAG = 2
+GRP_BUFS = 4
 RAW_BUFS = 6
 SINGLE_LOADS = 2
 V_AT = 3
 BIAS_STEP = 4
 OPEN_RATE = 2
-SCALAR_SHARE = 0.82
-EARLY_SHARE = 0.64
-EARLY_TO = 9
+SCALAR_SHARE = 0.86
+EARLY_SHARE = 0.7
+EARLY_TO = 10
 CODE_BUFS = 13
-LATE_SHARE = 0.7
+LATE_SHARE = 0.75
 END_SHARE = 0.35
 END_FROM = 24
 EXTRA_EVERY = 4
-EXTRA_FROM = 9
+EXTRA_FROM = 11
 EXTRA_NUM = 3
 OUT_BANKS = 6
-OPEN_FROM = 23
+OPEN_BEFORE = 1
+FQ = 3
+P_LATE = 4
+SLOW = 0
+SLOW_TO = 2
+P_EARLY = 2
+X_EARLY = 0
 OPEN_AGAIN = 33
 E_STEP = 0
 E_PHASE = 3
-C_STEP = 1
-C_PHASE = 1
+C_STEP = 0
+C_PHASE = 5
 Q_STEP = 1
 Q_PHASE = 3
 P_SPLIT = 2
@@ -68,7 +77,7 @@ X_DELAY = 1
 X_SPLIT = 2
 X_PHASE = 4
 VECTOR_OUT_FROM = 8
-FIRST_PRODUCT_STEP = 11
+FIRST_PRODUCT_STEP = 10
 
 
 def tile_fp4_value_cache_projection_s13_kernel(
@@ -78,8 +87,9 @@ def tile_fp4_value_cache_projection_s13_kernel(
     with ExitStack() as ctx:
         keep = ctx.enter_context(tc.tile_pool(name="keep", bufs=1))
         raw_pool = ctx.enter_context(tc.tile_pool(name="raw", bufs=RAW_BUFS))
-        grp_pool = ctx.enter_context(tc.tile_pool(name="grp", bufs=4))
+        grp_pool = ctx.enter_context(tc.tile_pool(name="grp", bufs=GRP_BUFS))
         code_pool = ctx.enter_context(tc.tile_pool(name="code", bufs=CODE_BUFS))
+        late_code_pool = ctx.enter_context(tc.tile_pool(name="late_code", bufs=4))
         small_pool = ctx.enter_context(tc.tile_pool(name="small", bufs=2))
         res_pool = ctx.enter_context(tc.tile_pool(name="res", bufs=4))
         head_psum = ctx.enter_context(tc.psum_pool(name="head_psum", bufs=1))
@@ -96,6 +106,7 @@ def tile_fp4_value_cache_projection_s13_kernel(
         bias_col = keep.tile([P, H * D // P], BF16)
         tok_rows = keep.tile([P, K_PASS], BF16)
         factor = keep.tile([P, UNITS, PACK], BF16)
+        first_factor = keep.tile([P, PACK], BF16)
         late_raw = [keep.tile([P, G, PACK, M], BF16, name="late_raw%d" % j) for j in range(LATE_HEADS)]
         o_rows = [keep.tile([P, QT, K_PASS], BF16, name="o_rows%d" % g) for g in range(G2)]
         o_first = keep.tile([P, M * PACK], BF16, align_bytes=64)
@@ -103,6 +114,7 @@ def tile_fp4_value_cache_projection_s13_kernel(
         o_first_plane = keep.tile([P, M], U8, align_bytes=64)
 
         raw = {}
+        pairs = {}
         grouped = {}
         a_code = {}
         a_plane = {}
@@ -151,6 +163,7 @@ def tile_fp4_value_cache_projection_s13_kernel(
                 pair = raw_tile[:]
             else:
                 pair = late_raw[h - EARLY_HEADS][:, g : g + 2]
+            pairs[k] = pair
             raw[2 * k] = pair[:, 0]
             raw[2 * k + 1] = pair[:, 1]
             rows = probs[h, g * K_PASS : (g + 2) * K_PASS, :].rearrange("(g p t) i -> p g t i", p=P, t=PACK)
@@ -177,35 +190,37 @@ def tile_fp4_value_cache_projection_s13_kernel(
             for t in range(PACK):
                 row = raw[i][:, t, :]
                 nc.vector.tensor_scalar(
-                    out=row, in0=row, scalar1=factor[:, i, t : t + 1], scalar2=None, op0=MULT
+                    out=row, in0=row, scalar1=(factor[:, i] if i > 0 else first_factor)[:, t : t + 1], scalar2=None, op0=MULT
                 )
 
         def interleave(u):
-            assert state['scaled'] > (u if u < LATE else LATE + G * LATE_ORDER[u - LATE][1] + 3), u
-            grp = grp_pool.tile([P, M * PACK], BF16, align_bytes=64)
+            first, count = units[u]
+            grp = grp_pool.tile([P, count * M * PACK], BF16, align_bytes=64)
             grouped[u] = grp
-            if u < LATE:
-                src = raw[u].rearrange("p t (c i) -> p c t i", i=RUN)
-                dst = grp[:].rearrange("p (c i t) -> p c t i", i=RUN, t=PACK)
-                runs = M // RUN
-                cut = int(runs * (SCALAR_SHARE if u >= EARLY_TO else EARLY_SHARE)) // 2 * 2
-                nc.scalar.copy(out=dst[:, :cut], in_=src[:, :cut])
-                nc.vector.tensor_copy(out=dst[:, cut:], in_=src[:, cut:])
+            if first < LATE:
+                assert state["scaled"] >= first + count
+                j = first % 2
+                src = pairs[first // 2][:, j : j + count]
+                share = SCALAR_SHARE if first >= EARLY_TO else EARLY_SHARE
             else:
-                q, j = LATE_ORDER[u - LATE]
-                src = late_raw[j][:, :, :, q * P : (q + 1) * P].rearrange("p g t (c i) -> p g c t i", i=RUN)
-                dst = grp[:].rearrange("p (g c i t) -> p g c t i", g=G, i=RUN, t=PACK)
-                runs = P // RUN
-                cut = int(runs * (LATE_SHARE if u < END_FROM else END_SHARE)) // 2 * 2
-                if cut > 0:
-                    nc.scalar.copy(out=dst[:, :, :cut], in_=src[:, :, :cut])
-                nc.vector.tensor_copy(out=dst[:, :, cut:], in_=src[:, :, cut:])
+                q, j = LATE_ORDER[first - LATE]
+                assert state["scaled"] >= LATE + G * (j + 1)
+                src = late_raw[j][:, :, :, q * P : (q + 1) * P]
+                share = LATE_SHARE if first < END_FROM else END_SHARE
+            src = src.rearrange("p g t (c i) -> p g c t i", i=RUN)
+            dst = grp[:].rearrange("p (g c i t) -> p g c t i", g=src.shape[1], i=RUN, t=PACK)
+            cut = int(src.shape[2] * share) // 2 * 2
+            nc.scalar.copy(out=dst[:, :, :cut], in_=src[:, :, :cut])
+            nc.vector.tensor_copy(out=dst[:, :, cut:], in_=src[:, :, cut:])
 
         def quantise(u):
-            code = code_pool.tile([P, M], U32, align_bytes=64)
-            plane = code_pool.tile([P, M], U8, align_bytes=64)
-            a_code[u] = code
-            a_plane[u] = plane
+            first, count = units[u]
+            pool = code_pool if first < LATE else late_code_pool
+            code = pool.tile([P, count * M], U32, align_bytes=64)
+            plane = pool.tile([P, count * M], U8, align_bytes=64)
+            for j in range(count):
+                a_code[first + j] = code[:, j * M : (j + 1) * M]
+                a_plane[first + j] = plane[:, j * M : (j + 1) * M]
             nc.vector.quantize_mx(out=code[:].bitcast(FP8X4), scales=plane[:], in_=grouped[u][:])
 
         def value_pass(dst, u, block, h, g):
@@ -259,8 +274,12 @@ def tile_fp4_value_cache_projection_s13_kernel(
 
         def first_turn(half):
             bank = turn_psum.tile([P, 2, 2, P], F32, tag="turn")
+            turned["first", half] = bank
             for j in range(2):
                 turn(bank[:, j], 0, 2 * half + j)
+
+        def first_copy(half):
+            bank = turned["first", half]
             dst = o_first[:, half * 2 * K_PASS : (half + 1) * 2 * K_PASS].bitcast(F32)
             nc.scalar.copy(
                 out=dst.rearrange("p (j q u) -> p j q u", j=2, u=2),
@@ -327,8 +346,9 @@ def tile_fp4_value_cache_projection_s13_kernel(
                     in_=staged[q, pair][:].rearrange("p j n -> p (j n)"),
                 )
 
-        nc.gpsimd.memset(tok_rows[32:64, :], 0.0)
-        nc.gpsimd.memset(tok_rows[64:, :], 0.0)
+        nc.scalar.dma_start(out=first_factor[:], in_=tok_scale[0, :K_PASS].rearrange("(p t) -> p t", t=PACK))
+        nc.vector.memset(tok_rows[32:64, :], 0.0)
+        nc.vector.memset(tok_rows[64:, :], 0.0)
         nc.scalar.dma_start(out=tok_rows[:UNITS, :], in_=tok_scale.rearrange("h (g k) -> (h g) k", g=G))
         nc.scalar.dma_start(out=bias_col[:], in_=v_bias.rearrange("(p c) -> p c", p=P))
         make_identity(nc, ident[:])
@@ -339,10 +359,16 @@ def tile_fp4_value_cache_projection_s13_kernel(
         loaded = RAW_BUFS
         spread_factor()
 
-        product_step = {max(G * h + G, FIRST_PRODUCT_STEP + 2 * h): h for h in range(EARLY_HEADS)}
-        first_pass_ready = max(s for s, h in product_step.items() if h == HEADS_PER_PASS - 1) + 1
-        closing_step = {LATE + LATE_ORDER.index((q, LATE_HEADS - 1)) + 1: q for q in range(QT)}
+        units = [(i, 1) for i in range(PAIR_FROM)] + [(i, 2) for i in range(PAIR_FROM, LATE, 2)]
+        late_unit = len(units)
+        units = units + [(i, 1) for i in range(LATE, UNITS)]
+        steps = len(units)
+        quantised = {first + j: u + 1 for u, (first, count) in enumerate(units) for j in range(count)}
+        product_step = {max(quantised[G * h + G - 1], quantised[FIRST_PRODUCT_STEP] + E_LAG * h): h for h in range(EARLY_HEADS)}
+        first_pass_ready = max(s for s, h in product_step.items() if h == HEADS_PER_PASS - 1) + E_LAG
+        closing_step = {late_unit + LATE_ORDER.index((q, LATE_HEADS - 1)) + 1: q for q in range(QT)}
         closes = sorted(closing_step)
+        last_add = max(product_step) + E_LAG
 
         plan = {}
 
@@ -366,52 +392,68 @@ def tile_fp4_value_cache_projection_s13_kernel(
             store(q, r)
             state["stored"] = state["stored"] + 1
 
-        for u in range(UNITS):
-            at(u + 1, 0, quantise, u)
+        for step, h in product_step.items():
+            at(step + E_LAG, 0 if step + E_LAG < closes[0] else -1, head_add_bias, h)
+        for u in range(steps):
+            at(u + 1, -1, quantise, u)
             if u >= 1:
                 at(u - 1, 2, interleave, u)
-            if u >= LATE:
-                q = LATE_ORDER[u - LATE][0]
-                free = closes[q - 1] if q > 0 else LATE + 1
-                if u + 1 > free:
-                    at(u + 1, 1, late_product, u)
-                else:
-                    at(free, 4, late_product, u)
+            if u >= late_unit:
+                i = units[u][0]
+                q = LATE_ORDER[i - LATE][0]
+                free = closes[q - 1] + 1 if q > 0 else last_add
+                at(max(u + 1, free), 1, late_product, i)
         for step, h in product_step.items():
             at(step, 1, head_product, h)
-            at(step + 1, 0, head_add_bias, h) if h < EARLY_HEADS - 1 else at(step + 1, 3, head_add_bias, h)
-        at(first_pass_ready + 1, 3, first_turn, 0)
-        at(first_pass_ready + 2, 3, first_turn, 1)
-        at(first_pass_ready + 4, 3, first_quantise)
-        at(BIAS_STEP, 3, spread_bias)
+        at(first_pass_ready, 3, first_turn, 0)
+        at(first_pass_ready + 1, 3, first_copy, 0)
+        at(first_pass_ready + 1, 3, first_turn, 1)
+        at(first_pass_ready + 2, 3, first_copy, 1)
+        at(first_pass_ready + FQ, 3, first_quantise)
+        at(quantised[BIAS_STEP], 3, spread_bias)
         for step, q in closing_step.items():
-            at(step, 3, late_add_bias, q)
-            at(step, 3, late_turn, q)
-            at(step, 5, late_copy, q)
-            at(step + 1, 3, late_quantise, q)
+            slow = SLOW if q < SLOW_TO else 0
+            at(step + slow, 0 if slow else 3, late_add_bias, q)
+            at(step + slow, 0 if slow else 3, late_turn, q)
+            if q == QT - 1:
+                at(step, 3, late_copy, q)
+            elif slow:
+                at(step + 1, 3, late_copy, q)
+            else:
+                at(step + C_STEP, C_PHASE, late_copy, q)
+            at(step + 1 + slow, 0 if slow else 3, late_quantise, q)
             for r in range(RT):
-                at(step + 1, 3, close_bank, q, r)
                 if q == QT - 2:
-                    at(closes[-1], 2 if r < 3 else 4, empty_bank, q, r)
+                    if r < P_EARLY:
+                        at(step + 1, 3, close_bank, q, r)
+                    else:
+                        at(closes[-1], 1 if r < P_LATE else 3, close_bank, q, r)
+                    if r < X_EARLY:
+                        at(closes[-1] - 1, 4, empty_bank, q, r)
+                    else:
+                        at(closes[-1], 2 if r < max(1, P_EARLY) else 4, empty_bank, q, r)
                 else:
+                    at(step + 1 + slow, 1 if slow else 3, close_bank, q, r)
                     at(step + 2, X_PHASE, empty_bank, q, r)
-        for s in range(OPEN_FROM, UNITS + 1):
-            at(s, 4 if s == closes[-1] else 3, open_banks, OPEN_RATE * (s - OPEN_FROM + 1) if s < closes[0] else QT * RT)
+        for s in range(closes[0] - OPEN_BEFORE, steps + 1):
+            at(s, 4 if s == closes[-1] else 3, open_banks, OPEN_RATE * (s - closes[0] + OPEN_BEFORE + 1) if s < closes[0] else (QT * RT if s >= closes[-1] else (QT - 1) * RT))
 
         scale_rows(0)
         interleave(0)
         scale_rows(1)
         scaled = 2
         state['scaled'] = 2
-        for s in range(UNITS + 6):
-            for phase in range(6):
+        for s in range(steps + 3):
+            for phase in range(-1, 6):
                 for job, args in plan.get((s, phase), []):
                     job(*args)
-            ahead = min(UNITS, s + 3 + max(0, (s - EXTRA_FROM) * EXTRA_NUM // EXTRA_EVERY + 1))
-            while loaded < min(UNITS // 2, (s + 2) // 2 + RAW_BUFS):
+            done = sum(count for first, count in units[: s + 2])
+            need = sum(count for first, count in units[: s + 3])
+            ahead = min(UNITS, need + max(0, (need - EXTRA_FROM) * EXTRA_NUM // EXTRA_EVERY))
+            while loaded < min(UNITS // 2, done // 2 + RAW_BUFS):
                 load_raw(loaded)
                 loaded = loaded + 1
             while scaled < ahead:
                 scale_rows(scaled)
                 scaled = scaled + 1
-                state['scaled'] = scaled
+                state["scaled"] = scaled

@@ -13,71 +13,31 @@ U32 = mybir.dt.uint32
 U8 = mybir.dt.uint8
 FP8X4 = mybir.dt.float8_e4m3fn_x4
 FP4X4 = mybir.dt.float4_e2m1fn_x4
-MULT = mybir.AluOpType.mult
-ADD = mybir.AluOpType.add
 
 P = 128
 PACK = 4
 K_PASS = P * PACK
 G = T // K_PASS
+G_OUT = H * D // K_PASS
+PASS_HEADS = K_PASS // D
 QT = M // P
-G2 = H * D // K_PASS
-HEADS_PER_PASS = K_PASS // D
 R_TILE = 512
 RT = N // R_TILE
-UNITS = H * G
+CHUNKS = H * G
 LATE_HEADS = 3
 EARLY_HEADS = H - LATE_HEADS
 LATE = EARLY_HEADS * G
 RUN = 4
-SKEW = 1
-LATE_ORDER = sorted(((q, j) for q in range(QT) for j in range(LATE_HEADS)), key=lambda e: (LATE_HEADS * e[0] + SKEW * e[1], e[0]))
 
-PAIR_FROM = 20
-E_LAG = 2
-GRP_BUFS = 4
-RAW_BUFS = 6
-SINGLE_LOADS = 2
-V_AT = 3
-BIAS_STEP = 4
-OPEN_RATE = 2
-SCALAR_SHARE = 0.86
-EARLY_SHARE = 0.7
-EARLY_TO = 10
-CODE_BUFS = 13
-LATE_SHARE = 0.75
-END_SHARE = 0.35
-END_FROM = 24
-EXTRA_EVERY = 4
-EXTRA_FROM = 11
-EXTRA_NUM = 3
+SHARE_START, SHARE_MAIN, SHARE_LATE, SHARE_END = 0.70, 0.86, 0.75, 0.35
+SCALE_AHEAD_FROM = 11
+FIRST_PRODUCT = 10
+
+PAIR_BUFS = 6
+UNIT_BUFS = 4
+CODE_BUFS = FIRST_PRODUCT + 3
 OUT_BANKS = 6
-OPEN_BEFORE = 1
-FQ = 3
-P_LATE = 4
-SLOW = 0
-SLOW_TO = 2
-P_EARLY = 2
-X_EARLY = 0
-OPEN_AGAIN = 33
-E_STEP = 0
-E_PHASE = 3
-C_STEP = 0
-C_PHASE = 5
-Q_STEP = 1
-Q_PHASE = 3
-P_SPLIT = 2
-P_STEP = 2
-P_PHASE = 2
-O_PHASE = 4
-RES_SPLIT = 12
-P_LAG = 0
-C_FIRST = 0
-X_DELAY = 1
-X_SPLIT = 2
-X_PHASE = 4
-VECTOR_OUT_FROM = 8
-FIRST_PRODUCT_STEP = 10
+LAG = 2
 
 
 def tile_fp4_value_cache_projection_s13_kernel(
@@ -86,11 +46,10 @@ def tile_fp4_value_cache_projection_s13_kernel(
     nc = tc.nc
     with ExitStack() as ctx:
         keep = ctx.enter_context(tc.tile_pool(name="keep", bufs=1))
-        raw_pool = ctx.enter_context(tc.tile_pool(name="raw", bufs=RAW_BUFS))
-        grp_pool = ctx.enter_context(tc.tile_pool(name="grp", bufs=GRP_BUFS))
+        pair_pool = ctx.enter_context(tc.tile_pool(name="pair", bufs=PAIR_BUFS))
+        unit_pool = ctx.enter_context(tc.tile_pool(name="unit", bufs=UNIT_BUFS))
         code_pool = ctx.enter_context(tc.tile_pool(name="code", bufs=CODE_BUFS))
-        late_code_pool = ctx.enter_context(tc.tile_pool(name="late_code", bufs=4))
-        small_pool = ctx.enter_context(tc.tile_pool(name="small", bufs=2))
+        o_pool = ctx.enter_context(tc.tile_pool(name="o", bufs=2))
         res_pool = ctx.enter_context(tc.tile_pool(name="res", bufs=4))
         head_psum = ctx.enter_context(tc.psum_pool(name="head_psum", bufs=1))
         turn_psum = ctx.enter_context(tc.psum_pool(name="turn_psum", bufs=1))
@@ -98,235 +57,205 @@ def tile_fp4_value_cache_projection_s13_kernel(
         ctx.enter_context(tc.manual_schedule())
 
         ident = keep.tile([P, P], F32)
-        v_code = keep.tile([P, G, 2 * H * D], U8, align_bytes=64)
-        v_plane = keep.tile([P, G, H * D], U8, align_bytes=64)
-        w_code = keep.tile([P, G2, 2 * N], U8, align_bytes=64)
-        w_plane = keep.tile([P, G2, N], U8, align_bytes=64)
+        v_code = [keep.tile([P, G, 2 * K_PASS], U8, align_bytes=64, name="v_code%d" % c) for c in range(G_OUT)]
+        v_plane = [keep.tile([P, G, K_PASS], U8, align_bytes=64, name="v_plane%d" % c) for c in range(G_OUT)]
+        w_code = [keep.tile([P, 2 * N], U8, align_bytes=64, name="w_code%d" % c) for c in range(G_OUT)]
+        w_plane = keep.tile([P, G_OUT, N], U8, align_bytes=64)
+        bias_rows = keep.tile([P, H * D // P], BF16)
         bias = keep.tile([P, H * D], BF16)
-        bias_col = keep.tile([P, H * D // P], BF16)
         tok_rows = keep.tile([P, K_PASS], BF16)
-        factor = keep.tile([P, UNITS, PACK], BF16)
+        factor = keep.tile([P, CHUNKS, PACK], BF16)
         first_factor = keep.tile([P, PACK], BF16)
-        late_raw = [keep.tile([P, G, PACK, M], BF16, name="late_raw%d" % j) for j in range(LATE_HEADS)]
-        o_rows = [keep.tile([P, QT, K_PASS], BF16, name="o_rows%d" % g) for g in range(G2)]
+        late_rows = [keep.tile([P, G, PACK, M], BF16, name="late_rows%d" % j) for j in range(LATE_HEADS)]
+        o_rows = [keep.tile([P, QT, K_PASS], BF16, name="o_rows%d" % c) for c in range(G_OUT)]
         o_first = keep.tile([P, M * PACK], BF16, align_bytes=64)
         o_first_code = keep.tile([P, M], U32, align_bytes=64)
         o_first_plane = keep.tile([P, M], U8, align_bytes=64)
 
-        raw = {}
-        pairs = {}
-        grouped = {}
-        a_code = {}
-        a_plane = {}
-        head_sum = {}
-        late_sum = {}
-        turned = {}
-        o_last = {}
-        o_last_code = {}
-        o_last_plane = {}
-        out_sum = {}
-        staged = {}
+        chunk, unit, a_code, a_plane, head_sum, turned = {}, {}, {}, {}, {}, {}
+        o_last, o_last_code, o_last_plane, out_sum, staged = {}, {}, {}, {}, {}
 
-        def spread_factor():
-            bank = turn_psum.tile([P, 2, 2, P], F32, tag="turn")
-            words = tok_rows[:].bitcast(F32)
-            for u in range(2):
-                nc.tensor.transpose(bank[:, 0, u, :], words[:, u : 2 * P : 2], ident[:])
-            nc.scalar.copy(out=factor[:].bitcast(F32), in_=bank[:, 0, :, :UNITS].rearrange("p u k -> p k u"))
-
-        def spread_bias():
-            bank = turn_psum.tile([P, 2, 2, P], F32, tag="turn")
-            cols = bank[:].rearrange("p a b n -> p (a b) n")
-            words = bias_col[:].bitcast(F32)
-            for c in range(4):
-                nc.tensor.transpose(cols[:, c, :], words[:, c : c + 1].to_broadcast([P, P]), ident[:])
-            nc.scalar.copy(
-                out=bias[:].bitcast(F32).rearrange("p (n c) -> p n c", c=4), in_=cols.rearrange("p c n -> p n c")
-            )
-
-        def load_words(dst, src, g0, g1):
-            nc.sync.dma_start(
-                out=dst[:, g0:g1, :].bitcast(I32), in_=src[g0:g1].rearrange("g p n -> p g n").bitcast(I32)
-            )
-
-        def load_plane(dst, src):
+        def load_plane(plane, scale_rows):
             for r in range(4):
                 nc.sync.dma_start(
-                    out=dst[r:P:32, :, :].bitcast(I32),
-                    in_=src[:, r:16:4, :].rearrange("g q n -> q g n").bitcast(I32),
+                    out=plane[r:P:32].bitcast(I32),
+                    in_=scale_rows[:, r:16:4, :].rearrange("g q n -> q g n").bitcast(I32),
                 )
 
-        def load_raw(k):
-            h, g = divmod(2 * k, G)
-            if 2 * k < LATE:
-                raw_tile = raw_pool.tile([P, 2, PACK, M], BF16)
-                pair = raw_tile[:]
-            else:
-                pair = late_raw[h - EARLY_HEADS][:, g : g + 2]
-            pairs[k] = pair
-            raw[2 * k] = pair[:, 0]
-            raw[2 * k + 1] = pair[:, 1]
-            rows = probs[h, g * K_PASS : (g + 2) * K_PASS, :].rearrange("(g p t) i -> p g t i", p=P, t=PACK)
-            if k < SINGLE_LOADS:
-                for j in range(2):
-                    if k == 0 and j == 0:
-                        nc.sync.dma_start(out=pair[:, j, :2], in_=rows[:, j, :2])
-                        nc.sync.dma_start(out=pair[:, j, 2:], in_=rows[:, j, 2:])
-                    else:
-                        nc.sync.dma_start(out=pair[:, j], in_=rows[:, j])
-            else:
-                nc.sync.dma_start(out=pair, in_=rows)
-            if k == V_AT:
-                load_words(v_code, v_words, 0, 2)
-            if k == V_AT + 1:
-                load_words(v_code, v_words, 2, 4)
-                load_plane(v_plane, v_scales)
-            if k == UNITS // 2 - 1:
-                load_plane(w_plane, wo_scales)
-                load_words(w_code, wo_words, 0, 1)
-                load_words(w_code, wo_words, 1, 2)
+        def load_values(c):
+            words = v_words[:, :, 2 * c * K_PASS : 2 * (c + 1) * K_PASS]
+            nc.sync.dma_start(out=v_code[c][:].bitcast(I32), in_=words.rearrange("g p n -> p g n").bitcast(I32))
+            load_plane(v_plane[c], v_scales[:, :, c * K_PASS : (c + 1) * K_PASS])
 
-        def scale_rows(i):
+        def load_pair(k):
+            h, g = divmod(2 * k, G)
+            if h < EARLY_HEADS:
+                pair_tile = pair_pool.tile([P, 2, PACK, M], BF16)
+                pair = pair_tile[:]
+            else:
+                pair = late_rows[h - EARLY_HEADS][:, g : g + 2]
+            chunk[2 * k] = pair[:, 0]
+            chunk[2 * k + 1] = pair[:, 1]
+            rows = probs[h, g * K_PASS : (g + 2) * K_PASS, :].rearrange("(g p t) i -> p g t i", p=P, t=PACK)
+            if k == 0:
+                pieces = [(0, slice(0, 2)), (0, slice(2, 4)), (1, slice(0, 4))]
+            elif k == 1:
+                pieces = [(0, slice(0, 4)), (1, slice(0, 4))]
+            else:
+                pieces = [(slice(0, 2), slice(0, 4))]
+            for j, t in pieces:
+                nc.sync.dma_start(out=pair[:, j, t], in_=rows[:, j, t])
+            if k == FIRST_PRODUCT // 2 - 1:
+                load_values(0)
+            if k == CHUNKS // 2 - 1:
+                load_values(1)
+                load_plane(w_plane, wo_scales)
+                for c in range(G_OUT):
+                    nc.sync.dma_start(out=w_code[c][:].bitcast(I32), in_=wo_words[c].bitcast(I32))
+
+        def spread_factor():
+            bank = turn_psum.tile([P, PACK, P], F32, tag="turn")
+            words = tok_rows[:].bitcast(F32)
+            for u in range(2):
+                nc.tensor.transpose(bank[:, u, :], words[:, u : 2 * P : 2], ident[:])
+            nc.scalar.copy(out=factor[:].bitcast(F32), in_=bank[:, :2, :CHUNKS].rearrange("p u c -> p c u"))
+
+        def spread_bias():
+            bank = turn_psum.tile([P, PACK, P], F32, tag="turn")
+            words = bias_rows[:].bitcast(F32)
+            for c in range(PACK):
+                nc.tensor.transpose(bank[:, c, :], words[:, c : c + 1].to_broadcast([P, P]), ident[:])
+            nc.scalar.copy(
+                out=bias[:].bitcast(F32).rearrange("p (n c) -> p n c", c=PACK),
+                in_=bank[:].rearrange("p c n -> p n c"),
+            )
+
+        def scale_chunk(i):
+            factors = first_factor if i == 0 else factor[:, i]
             for t in range(PACK):
-                row = raw[i][:, t, :]
+                row = chunk[i][:, t, :]
                 nc.vector.tensor_scalar(
-                    out=row, in0=row, scalar1=(factor[:, i] if i > 0 else first_factor)[:, t : t + 1], scalar2=None, op0=MULT
+                    out=row, in0=row, scalar1=factors[:, t : t + 1], scalar2=None, op0=mybir.AluOpType.mult
                 )
 
         def interleave(u):
-            first, count = units[u]
-            grp = grp_pool.tile([P, count * M * PACK], BF16, align_bytes=64)
-            grouped[u] = grp
-            if first < LATE:
-                assert state["scaled"] >= first + count
-                j = first % 2
-                src = pairs[first // 2][:, j : j + count]
-                share = SCALAR_SHARE if first >= EARLY_TO else EARLY_SHARE
+            unit_tile = unit_pool.tile([P, M * PACK], BF16, align_bytes=64)
+            unit[u] = unit_tile
+            if u < LATE:
+                src = chunk[u].unsqueeze(1)
+                share = SHARE_START if u < FIRST_PRODUCT else SHARE_MAIN
             else:
-                q, j = LATE_ORDER[first - LATE]
-                assert state["scaled"] >= LATE + G * (j + 1)
-                src = late_raw[j][:, :, :, q * P : (q + 1) * P]
-                share = LATE_SHARE if first < END_FROM else END_SHARE
+                q, j = divmod(u - LATE, LATE_HEADS)
+                src = late_rows[j][:, :, :, q * P : (q + 1) * P]
+                share = SHARE_LATE if u <= LATE + LATE_HEADS else SHARE_END
             src = src.rearrange("p g t (c i) -> p g c t i", i=RUN)
-            dst = grp[:].rearrange("p (g c i t) -> p g c t i", g=src.shape[1], i=RUN, t=PACK)
+            dst = unit_tile[:].rearrange("p (g c i t) -> p g c t i", g=src.shape[1], i=RUN, t=PACK)
             cut = int(src.shape[2] * share) // 2 * 2
             nc.scalar.copy(out=dst[:, :, :cut], in_=src[:, :, :cut])
             nc.vector.tensor_copy(out=dst[:, :, cut:], in_=src[:, :, cut:])
 
         def quantise(u):
-            first, count = units[u]
-            pool = code_pool if first < LATE else late_code_pool
-            code = pool.tile([P, count * M], U32, align_bytes=64)
-            plane = pool.tile([P, count * M], U8, align_bytes=64)
-            for j in range(count):
-                a_code[first + j] = code[:, j * M : (j + 1) * M]
-                a_plane[first + j] = plane[:, j * M : (j + 1) * M]
-            nc.vector.quantize_mx(out=code[:].bitcast(FP8X4), scales=plane[:], in_=grouped[u][:])
+            code = code_pool.tile([P, M], U32, align_bytes=64)
+            plane = code_pool.tile([P, M], U8, align_bytes=64)
+            a_code[u] = code
+            a_plane[u] = plane
+            nc.vector.quantize_mx(out=code[:].bitcast(FP8X4), scales=plane[:], in_=unit[u][:])
 
         def value_pass(dst, u, block, h, g):
+            c, j = divmod(h, PASS_HEADS)
             cols = slice(block * P, (block + 1) * P)
             nc.tensor.matmul_mx(
                 out=dst,
                 lhsT=a_code[u][:, cols].bitcast(FP8X4),
                 lhsT_scale=a_plane[u][:, cols],
-                rhs=v_code[:, g, 2 * h * D : 2 * (h + 1) * D].bitcast(FP4X4),
-                rhs_scale=v_plane[:, g, h * D : (h + 1) * D],
+                rhs=v_code[c][:, g, 2 * j * D : 2 * (j + 1) * D].bitcast(FP4X4),
+                rhs_scale=v_plane[c][:, g, j * D : (j + 1) * D],
                 start=(g == 0),
                 stop=(g == G - 1),
             )
 
-        def head_product(h):
-            acc = head_psum.tile([P, QT, D], F32, tag="head")
-            head_sum[h] = acc
+        def early_product(h):
+            sums = head_psum.tile([P, QT, D], F32, tag="head")
+            head_sum[h] = sums
             for q in range(QT):
                 for g in range(G):
-                    value_pass(acc[:, q, :], h * G + g, q, h, g)
+                    value_pass(sums[:, q, :], h * G + g, q, h, g)
 
-        def head_add_bias(h):
-            g2, j = divmod(h, HEADS_PER_PASS)
+        def early_add_bias(h):
+            c, j = divmod(h, PASS_HEADS)
             nc.vector.tensor_tensor(
-                out=o_rows[g2][:, :, j * D : (j + 1) * D],
+                out=o_rows[c][:, :, j * D : (j + 1) * D],
                 in0=head_sum[h][:],
                 in1=bias[:, h * D : (h + 1) * D].unsqueeze(1).to_broadcast([P, QT, D]),
-                op=ADD,
+                op=mybir.AluOpType.add,
             )
 
         def late_product(u):
-            q, j = LATE_ORDER[u - LATE]
+            q, j = divmod(u - LATE, LATE_HEADS)
             if j == 0:
-                acc = head_psum.tile([P, QT, D], F32, tag="head")
-                late_sum[q] = acc
+                sums = head_psum.tile([P, QT, D], F32, tag="head")
+                head_sum["late", q] = sums
             for g in range(G):
-                value_pass(late_sum[q][:, j, :], u, g, EARLY_HEADS + j, g)
+                value_pass(head_sum["late", q][:, j, :], u, g, EARLY_HEADS + j, g)
 
         def late_add_bias(q):
             nc.vector.tensor_tensor(
-                out=o_rows[G2 - 1][:, q, K_PASS - LATE_HEADS * D :],
-                in0=late_sum[q][:, :LATE_HEADS, :].rearrange("p j d -> p (j d)"),
+                out=o_rows[G_OUT - 1][:, q, K_PASS - LATE_HEADS * D :],
+                in0=head_sum["late", q][:, :LATE_HEADS, :].rearrange("p j d -> p (j d)"),
                 in1=bias[:, EARLY_HEADS * D :],
-                op=ADD,
+                op=mybir.AluOpType.add,
             )
 
-        def turn(dst, g2, q):
-            words = o_rows[g2][:, q, :].bitcast(F32)
-            for u in range(2):
-                nc.tensor.transpose(dst[:, u, :], words[:, u : 2 * P : 2], ident[:])
+        def turn(c, tiles):
+            bank = turn_psum.tile([P, PACK, P], F32, tag="turn")
+            turned[c, tiles[0]] = bank
+            for n, q in enumerate(tiles):
+                words = o_rows[c][:, q, :].bitcast(F32)
+                for u in range(2):
+                    nc.tensor.transpose(bank[:, 2 * n + u, :], words[:, u : 2 * P : 2], ident[:])
 
-        def first_turn(half):
-            bank = turn_psum.tile([P, 2, 2, P], F32, tag="turn")
-            turned["first", half] = bank
-            for j in range(2):
-                turn(bank[:, j], 0, 2 * half + j)
-
-        def first_copy(half):
-            bank = turned["first", half]
-            dst = o_first[:, half * 2 * K_PASS : (half + 1) * 2 * K_PASS].bitcast(F32)
+        def first_copy(q):
+            dst = o_first[:, q * K_PASS : (q + 2) * K_PASS].bitcast(F32)
             nc.scalar.copy(
-                out=dst.rearrange("p (j q u) -> p j q u", j=2, u=2),
-                in_=bank[:].rearrange("p j u q -> p j q u"),
+                out=dst.rearrange("p (n i u) -> p n i u", n=2, u=2),
+                in_=turned[0, q][:].rearrange("p (n u) i -> p n i u", u=2),
             )
 
-        def first_quantise():
-            nc.vector.quantize_mx(out=o_first_code[:].bitcast(FP8X4), scales=o_first_plane[:], in_=o_first[:])
-
-        def late_turn(q):
-            bank = turn_psum.tile([P, 2, 2, P], F32, tag="turn")
-            turned[q] = bank
-            turn(bank[:, 0], G2 - 1, q)
-
-        def late_copy(q):
-            o_tile = small_pool.tile([P, K_PASS], BF16, align_bytes=64)
+        def last_copy(q):
+            o_tile = o_pool.tile([P, K_PASS], BF16, align_bytes=64)
             o_last[q] = o_tile
             nc.scalar.copy(
-                out=o_tile[:].bitcast(F32).rearrange("p (q u) -> p q u", u=2),
-                in_=turned[q][:, 0].rearrange("p u q -> p q u"),
+                out=o_tile[:].bitcast(F32).rearrange("p (i u) -> p i u", u=2),
+                in_=turned[G_OUT - 1, q][:, :2, :].rearrange("p u i -> p i u"),
             )
 
-        def late_quantise(q):
-            o_code = small_pool.tile([P, P], U32, align_bytes=64)
-            o_plane = small_pool.tile([P, P], U8, align_bytes=64)
+        def last_quantise(q):
+            o_code = o_pool.tile([P, P], U32, align_bytes=64)
+            o_plane = o_pool.tile([P, P], U8, align_bytes=64)
             o_last_code[q] = o_code
             o_last_plane[q] = o_plane
             nc.vector.quantize_mx(out=o_code[:].bitcast(FP8X4), scales=o_plane[:], in_=o_last[q][:])
 
-        def project(q, r, g2):
-            if g2 == 0:
-                acc = out_psum.tile([P, R_TILE], F32, tag="out")
-                out_sum[q, r] = acc
-                code = o_first_code[:, q * P : (q + 1) * P]
-                plane = o_first_plane[:, q * P : (q + 1) * P]
+        def project(q, r, c):
+            if c == 0:
+                sums = out_psum.tile([P, R_TILE], F32, tag="out")
+                out_sum[q, r] = sums
+                code, plane = o_first_code[:, q * P : (q + 1) * P], o_first_plane[:, q * P : (q + 1) * P]
             else:
-                code = o_last_code[q][:]
-                plane = o_last_plane[q][:]
+                code, plane = o_last_code[q][:], o_last_plane[q][:]
             nc.tensor.matmul_mx(
                 out=out_sum[q, r][:],
                 lhsT=code.bitcast(FP8X4),
                 lhsT_scale=plane,
-                rhs=w_code[:, g2, 2 * r * R_TILE : 2 * (r + 1) * R_TILE].bitcast(FP4X4),
-                rhs_scale=w_plane[:, g2, r * R_TILE : (r + 1) * R_TILE],
-                start=(g2 == 0),
-                stop=(g2 == G2 - 1),
+                rhs=w_code[c][:, 2 * r * R_TILE : 2 * (r + 1) * R_TILE].bitcast(FP4X4),
+                rhs_scale=w_plane[:, c, r * R_TILE : (r + 1) * R_TILE],
+                start=(c == 0),
+                stop=(c == G_OUT - 1),
             )
+
+        def open_banks(count):
+            for n in range(len(out_sum), count):
+                project(n // RT, n % RT, 0)
 
         def store(q, r):
             pair, j = divmod(r, 2)
@@ -334,126 +263,102 @@ def tile_fp4_value_cache_projection_s13_kernel(
                 res = res_pool.tile([P, 2, R_TILE], F32)
                 staged[q, pair] = res
             dst = staged[q, pair][:, j, :]
-            if q * RT + r >= VECTOR_OUT_FROM and r % 2 == 1:
+            if q >= QT - 2 and j == 1:
                 nc.vector.tensor_copy(out=dst, in_=out_sum[q, r][:])
             else:
                 nc.scalar.copy(out=dst, in_=out_sum[q, r][:])
-            if q * RT + r >= RES_SPLIT:
-                nc.sync.dma_start(out=out[q * P : (q + 1) * P, r * R_TILE : (r + 1) * R_TILE], in_=dst)
+            rows = slice(q * P, (q + 1) * P)
+            if q == QT - 1:
+                nc.sync.dma_start(out=out[rows, r * R_TILE : (r + 1) * R_TILE], in_=dst)
             elif j == 1:
                 nc.sync.dma_start(
-                    out=out[q * P : (q + 1) * P, pair * 2 * R_TILE : (pair + 1) * 2 * R_TILE],
+                    out=out[rows, (r - 1) * R_TILE : (r + 1) * R_TILE],
                     in_=staged[q, pair][:].rearrange("p j n -> p (j n)"),
                 )
 
         nc.scalar.dma_start(out=first_factor[:], in_=tok_scale[0, :K_PASS].rearrange("(p t) -> p t", t=PACK))
         nc.vector.memset(tok_rows[32:64, :], 0.0)
         nc.vector.memset(tok_rows[64:, :], 0.0)
-        nc.scalar.dma_start(out=tok_rows[:UNITS, :], in_=tok_scale.rearrange("h (g k) -> (h g) k", g=G))
-        nc.scalar.dma_start(out=bias_col[:], in_=v_bias.rearrange("(p c) -> p c", p=P))
+        nc.scalar.dma_start(out=tok_rows[:CHUNKS, :], in_=tok_scale.rearrange("h (g k) -> (h g) k", g=G))
+        nc.scalar.dma_start(out=bias_rows[:], in_=v_bias.rearrange("(p c) -> p c", p=P))
         make_identity(nc, ident[:])
-        nc.vector.memset(v_plane[:].bitcast(U32), 0)
-        nc.vector.memset(w_plane[:].bitcast(U32), 0)
-        for k in range(RAW_BUFS):
-            load_raw(k)
-        loaded = RAW_BUFS
+        for plane in v_plane + [w_plane]:
+            nc.vector.memset(plane[:].bitcast(U32), 0)
+        for k in range(PAIR_BUFS):
+            load_pair(k)
         spread_factor()
 
-        units = [(i, 1) for i in range(PAIR_FROM)] + [(i, 2) for i in range(PAIR_FROM, LATE, 2)]
-        late_unit = len(units)
-        units = units + [(i, 1) for i in range(LATE, UNITS)]
-        steps = len(units)
-        quantised = {first + j: u + 1 for u, (first, count) in enumerate(units) for j in range(count)}
-        product_step = {max(quantised[G * h + G - 1], quantised[FIRST_PRODUCT_STEP] + E_LAG * h): h for h in range(EARLY_HEADS)}
-        first_pass_ready = max(s for s, h in product_step.items() if h == HEADS_PER_PASS - 1) + E_LAG
-        closing_step = {late_unit + LATE_ORDER.index((q, LATE_HEADS - 1)) + 1: q for q in range(QT)}
-        closes = sorted(closing_step)
-        last_add = max(product_step) + E_LAG
+        product_step = {max(G * (h + 1), FIRST_PRODUCT + LAG * h): h for h in range(EARLY_HEADS)}
+        first_done = G * PASS_HEADS + LAG
+        head_free = LATE + LAG
+        closing = {LATE + LATE_HEADS * (q + 1): q for q in range(QT)}
+        last_step = CHUNKS
+        held = QT - 2
 
-        plan = {}
-
-        def at(step, phase, job, *args):
-            plan.setdefault((step, phase), []).append((job, args))
-
-        state = {"opened": 0, "stored": 0, "scaled": 1}
-
-        def open_banks(limit):
-            while state["opened"] < min(limit, state["stored"] + OUT_BANKS):
-                project(*divmod(state["opened"], RT), 0)
-                state["opened"] = state["opened"] + 1
-
-        def close_bank(q, r):
-            while state["opened"] <= q * RT + r:
-                project(*divmod(state["opened"], RT), 0)
-                state["opened"] = state["opened"] + 1
-            project(q, r, 1)
-
-        def empty_bank(q, r):
-            store(q, r)
-            state["stored"] = state["stored"] + 1
-
-        for step, h in product_step.items():
-            at(step + E_LAG, 0 if step + E_LAG < closes[0] else -1, head_add_bias, h)
-        for u in range(steps):
-            at(u + 1, -1, quantise, u)
-            if u >= 1:
-                at(u - 1, 2, interleave, u)
-            if u >= late_unit:
-                i = units[u][0]
-                q = LATE_ORDER[i - LATE][0]
-                free = closes[q - 1] + 1 if q > 0 else last_add
-                at(max(u + 1, free), 1, late_product, i)
-        for step, h in product_step.items():
-            at(step, 1, head_product, h)
-        at(first_pass_ready, 3, first_turn, 0)
-        at(first_pass_ready + 1, 3, first_copy, 0)
-        at(first_pass_ready + 1, 3, first_turn, 1)
-        at(first_pass_ready + 2, 3, first_copy, 1)
-        at(first_pass_ready + FQ, 3, first_quantise)
-        at(quantised[BIAS_STEP], 3, spread_bias)
-        for step, q in closing_step.items():
-            slow = SLOW if q < SLOW_TO else 0
-            at(step + slow, 0 if slow else 3, late_add_bias, q)
-            at(step + slow, 0 if slow else 3, late_turn, q)
-            if q == QT - 1:
-                at(step, 3, late_copy, q)
-            elif slow:
-                at(step + 1, 3, late_copy, q)
-            else:
-                at(step + C_STEP, C_PHASE, late_copy, q)
-            at(step + 1 + slow, 0 if slow else 3, late_quantise, q)
-            for r in range(RT):
-                if q == QT - 2:
-                    if r < P_EARLY:
-                        at(step + 1, 3, close_bank, q, r)
-                    else:
-                        at(closes[-1], 1 if r < P_LATE else 3, close_bank, q, r)
-                    if r < X_EARLY:
-                        at(closes[-1] - 1, 4, empty_bank, q, r)
-                    else:
-                        at(closes[-1], 2 if r < max(1, P_EARLY) else 4, empty_bank, q, r)
-                else:
-                    at(step + 1 + slow, 1 if slow else 3, close_bank, q, r)
-                    at(step + 2, X_PHASE, empty_bank, q, r)
-        for s in range(closes[0] - OPEN_BEFORE, steps + 1):
-            at(s, 4 if s == closes[-1] else 3, open_banks, OPEN_RATE * (s - closes[0] + OPEN_BEFORE + 1) if s < closes[0] else (QT * RT if s >= closes[-1] else (QT - 1) * RT))
-
-        scale_rows(0)
+        scale_chunk(0)
         interleave(0)
-        scale_rows(1)
-        scaled = 2
-        state['scaled'] = 2
-        for s in range(steps + 3):
-            for phase in range(-1, 6):
-                for job, args in plan.get((s, phase), []):
-                    job(*args)
-            done = sum(count for first, count in units[: s + 2])
-            need = sum(count for first, count in units[: s + 3])
-            ahead = min(UNITS, need + max(0, (need - EXTRA_FROM) * EXTRA_NUM // EXTRA_EVERY))
-            while loaded < min(UNITS // 2, done // 2 + RAW_BUFS):
-                load_raw(loaded)
+        scale_chunk(1)
+        scaled, loaded = 2, PAIR_BUFS
+        for s in range(last_step + 1):
+            if s >= 1:
+                quantise(s - 1)
+            if s - LAG in product_step:
+                early_add_bias(product_step[s - LAG])
+            if s == head_free:
+                for u in range(LATE, s - 1):
+                    late_product(u)
+            if s >= head_free:
+                late_product(s - 1)
+            if s in product_step:
+                early_product(product_step[s])
+            if s == last_step:
+                for r in range(2, RT):
+                    project(held, r, 1)
+                for r in range(RT - 1):
+                    store(held, r)
+            if s + 1 < CHUNKS:
+                interleave(s + 1)
+
+            if s == FIRST_PRODUCT // 2:
+                spread_bias()
+            if s == first_done + 1:
+                first_copy(0)
+            if s in (first_done, first_done + 1):
+                turn(0, [2 * (s - first_done), 2 * (s - first_done) + 1])
+            if s == first_done + 2:
+                first_copy(2)
+            if s == first_done + 3:
+                nc.vector.quantize_mx(out=o_first_code[:].bitcast(FP8X4), scales=o_first_plane[:], in_=o_first[:])
+
+            if s in closing:
+                late_add_bias(closing[s])
+                turn(G_OUT - 1, [closing[s]])
+            if s - 1 in closing:
+                q = closing[s - 1]
+                last_quantise(q)
+                for r in range(2 if q == held else RT):
+                    project(q, r, 1)
+            if s + 1 in closing and s + 1 < last_step:
+                open_banks(RT * closing[s + 1] + 2)
+            if s in closing and s < last_step:
+                open_banks(RT * (closing[s] + 1))
+            if s - 2 in closing and closing[s - 2] < held:
+                for r in range(RT):
+                    store(closing[s - 2], r)
+            if s in closing:
+                last_copy(closing[s])
+
+            while loaded < min(CHUNKS // 2, (s + 2) // 2 + PAIR_BUFS):
+                load_pair(loaded)
                 loaded = loaded + 1
-            while scaled < ahead:
-                scale_rows(scaled)
+            while scaled < min(CHUNKS, s + 3 + max(0, (s + 3 - SCALE_AHEAD_FROM) * 3 // 4)):
+                scale_chunk(scaled)
                 scaled = scaled + 1
-                state["scaled"] = scaled
+
+        store(held, RT - 1)
+        open_banks(QT * RT)
+        last_quantise(QT - 1)
+        for r in range(RT):
+            project(QT - 1, r, 1)
+        for r in range(RT):
+            store(QT - 1, r)

@@ -27,7 +27,7 @@ CHUNKS = H * G
 LATE_HEADS = 3
 EARLY_HEADS = H - LATE_HEADS
 LATE = EARLY_HEADS * G
-RUN = 4
+RUN = 2
 
 SHARE_START, SHARE_MAIN, SHARE_LATE, SHARE_END = 0.70, 0.86, 0.75, 0.35
 SCALE_AHEAD_FROM = 11

from contextlib import ExitStack

import concourse.mybir as mybir
from concourse.masks import make_identity

H, D, T, M, N = 8, 128, 2048, 512, 2048
FLOPS = 2 * H * D * T * M + 2 * M * H * D * N

F32 = mybir.dt.float32
BF16 = mybir.dt.bfloat16
I32 = mybir.dt.int32
U32 = mybir.dt.uint32
U8 = mybir.dt.uint8
FP8X4 = mybir.dt.float8_e4m3fn_x4
FP4X4 = mybir.dt.float4_e2m1fn_x4

P = 128
PACK = 4
K_PASS = P * PACK
G = T // K_PASS
G_OUT = H * D // K_PASS
PASS_HEADS = K_PASS // D
QT = M // P
R_TILE = 512
RT = N // R_TILE
CHUNKS = H * G
LATE_HEADS = 3
EARLY_HEADS = H - LATE_HEADS
LATE = EARLY_HEADS * G
RUN = 2

SHARE_START, SHARE_MAIN, SHARE_LATE, SHARE_END = 0.70, 0.86, 0.75, 0.35
SCALE_AHEAD_FROM = 11
FIRST_PRODUCT = 10

PAIR_BUFS = 6
UNIT_BUFS = 4
CODE_BUFS = FIRST_PRODUCT + 3
OUT_BANKS = 6
LAG = 2


def tile_fp4_value_cache_projection_s13_kernel(
    tc, probs, tok_scale, v_words, v_scales, v_bias, wo_words, wo_scales, out
):
    nc = tc.nc
    with ExitStack() as ctx:
        keep = ctx.enter_context(tc.tile_pool(name="keep", bufs=1))
        pair_pool = ctx.enter_context(tc.tile_pool(name="pair", bufs=PAIR_BUFS))
        unit_pool = ctx.enter_context(tc.tile_pool(name="unit", bufs=UNIT_BUFS))
        code_pool = ctx.enter_context(tc.tile_pool(name="code", bufs=CODE_BUFS))
        o_pool = ctx.enter_context(tc.tile_pool(name="o", bufs=2))
        res_pool = ctx.enter_context(tc.tile_pool(name="res", bufs=4))
        head_psum = ctx.enter_context(tc.psum_pool(name="head_psum", bufs=1))
        turn_psum = ctx.enter_context(tc.psum_pool(name="turn_psum", bufs=1))
        out_psum = ctx.enter_context(tc.psum_pool(name="out_psum", bufs=OUT_BANKS))
        ctx.enter_context(tc.manual_schedule())

        ident = keep.tile([P, P], F32)
        v_code = [keep.tile([P, G, 2 * K_PASS], U8, align_bytes=64, name="v_code%d" % c) for c in range(G_OUT)]
        v_plane = [keep.tile([P, G, K_PASS], U8, align_bytes=64, name="v_plane%d" % c) for c in range(G_OUT)]
        w_code = [keep.tile([P, 2 * N], U8, align_bytes=64, name="w_code%d" % c) for c in range(G_OUT)]
        w_plane = keep.tile([P, G_OUT, N], U8, align_bytes=64)
        bias_rows = keep.tile([P, H * D // P], BF16)
        bias = keep.tile([P, H * D], BF16)
        tok_rows = keep.tile([P, K_PASS], BF16)
        factor = keep.tile([P, CHUNKS, PACK], BF16)
        first_factor = keep.tile([P, PACK], BF16)
        late_rows = [keep.tile([P, G, PACK, M], BF16, name="late_rows%d" % j) for j in range(LATE_HEADS)]
        o_rows = [keep.tile([P, QT, K_PASS], BF16, name="o_rows%d" % c) for c in range(G_OUT)]
        o_first = keep.tile([P, M * PACK], BF16, align_bytes=64)
        o_first_code = keep.tile([P, M], U32, align_bytes=64)
        o_first_plane = keep.tile([P, M], U8, align_bytes=64)

        chunk, unit, a_code, a_plane, head_sum, turned = {}, {}, {}, {}, {}, {}
        o_last, o_last_code, o_last_plane, out_sum, staged = {}, {}, {}, {}, {}

        def load_plane(plane, scale_rows):
            for r in range(4):
                nc.sync.dma_start(
                    out=plane[r:P:32].bitcast(I32),
                    in_=scale_rows[:, r:16:4, :].rearrange("g q n -> q g n").bitcast(I32),
                )

        def load_values(c):
            words = v_words[:, :, 2 * c * K_PASS : 2 * (c + 1) * K_PASS]
            nc.sync.dma_start(out=v_code[c][:].bitcast(I32), in_=words.rearrange("g p n -> p g n").bitcast(I32))
            load_plane(v_plane[c], v_scales[:, :, c * K_PASS : (c + 1) * K_PASS])

        def load_pair(k):
            h, g = divmod(2 * k, G)
            if h < EARLY_HEADS:
                pair_tile = pair_pool.tile([P, 2, PACK, M], BF16)
                pair = pair_tile[:]
            else:
                pair = late_rows[h - EARLY_HEADS][:, g : g + 2]
            chunk[2 * k] = pair[:, 0]
            chunk[2 * k + 1] = pair[:, 1]
            rows = probs[h, g * K_PASS : (g + 2) * K_PASS, :].rearrange("(g p t) i -> p g t i", p=P, t=PACK)
            if k == 0:
                pieces = [(0, slice(0, 2)), (0, slice(2, 4)), (1, slice(0, 4))]
            elif k == 1:
                pieces = [(0, slice(0, 4)), (1, slice(0, 4))]
            else:
                pieces = [(slice(0, 2), slice(0, 4))]
            for j, t in pieces:
                nc.sync.dma_start(out=pair[:, j, t], in_=rows[:, j, t])
            if k == FIRST_PRODUCT // 2 - 1:
                load_values(0)
            if k == CHUNKS // 2 - 1:
                load_values(1)
                load_plane(w_plane, wo_scales)
                for c in range(G_OUT):
                    nc.sync.dma_start(out=w_code[c][:].bitcast(I32), in_=wo_words[c].bitcast(I32))

        def spread_factor():
            bank = turn_psum.tile([P, PACK, P], F32, tag="turn")
            words = tok_rows[:].bitcast(F32)
            for u in range(2):
                nc.tensor.transpose(bank[:, u, :], words[:, u : 2 * P : 2], ident[:])
            nc.scalar.copy(out=factor[:].bitcast(F32), in_=bank[:, :2, :CHUNKS].rearrange("p u c -> p c u"))

        def spread_bias():
            bank = turn_psum.tile([P, PACK, P], F32, tag="turn")
            words = bias_rows[:].bitcast(F32)
            for c in range(PACK):
                nc.tensor.transpose(bank[:, c, :], words[:, c : c + 1].to_broadcast([P, P]), ident[:])
            nc.scalar.copy(
                out=bias[:].bitcast(F32).rearrange("p (n c) -> p n c", c=PACK),
                in_=bank[:].rearrange("p c n -> p n c"),
            )

        def scale_chunk(i):
            factors = first_factor if i == 0 else factor[:, i]
            for t in range(PACK):
                row = chunk[i][:, t, :]
                nc.vector.tensor_scalar(
                    out=row, in0=row, scalar1=factors[:, t : t + 1], scalar2=None, op0=mybir.AluOpType.mult
                )

        def interleave(u):
            unit_tile = unit_pool.tile([P, M * PACK], BF16, align_bytes=64)
            unit[u] = unit_tile
            if u < LATE:
                src = chunk[u].unsqueeze(1)
                share = SHARE_START if u < FIRST_PRODUCT else SHARE_MAIN
            else:
                q, j = divmod(u - LATE, LATE_HEADS)
                src = late_rows[j][:, :, :, q * P : (q + 1) * P]
                share = SHARE_LATE if u <= LATE + LATE_HEADS else SHARE_END
            src = src.rearrange("p g t (c i) -> p g c t i", i=RUN)
            dst = unit_tile[:].rearrange("p (g c i t) -> p g c t i", g=src.shape[1], i=RUN, t=PACK)
            cut = int(src.shape[2] * share) // 2 * 2
            nc.scalar.copy(out=dst[:, :, :cut], in_=src[:, :, :cut])
            nc.vector.tensor_copy(out=dst[:, :, cut:], in_=src[:, :, cut:])

        def quantise(u):
            code = code_pool.tile([P, M], U32, align_bytes=64)
            plane = code_pool.tile([P, M], U8, align_bytes=64)
            a_code[u] = code
            a_plane[u] = plane
            nc.vector.quantize_mx(out=code[:].bitcast(FP8X4), scales=plane[:], in_=unit[u][:])

        def value_pass(dst, u, block, h, g):
            c, j = divmod(h, PASS_HEADS)
            cols = slice(block * P, (block + 1) * P)
            nc.tensor.matmul_mx(
                out=dst,
                lhsT=a_code[u][:, cols].bitcast(FP8X4),
                lhsT_scale=a_plane[u][:, cols],
                rhs=v_code[c][:, g, 2 * j * D : 2 * (j + 1) * D].bitcast(FP4X4),
                rhs_scale=v_plane[c][:, g, j * D : (j + 1) * D],
                start=(g == 0),
                stop=(g == G - 1),
            )

        def early_product(h):
            sums = head_psum.tile([P, QT, D], F32, tag="head")
            head_sum[h] = sums
            for q in range(QT):
                for g in range(G):
                    value_pass(sums[:, q, :], h * G + g, q, h, g)

        def early_add_bias(h):
            c, j = divmod(h, PASS_HEADS)
            nc.vector.tensor_tensor(
                out=o_rows[c][:, :, j * D : (j + 1) * D],
                in0=head_sum[h][:],
                in1=bias[:, h * D : (h + 1) * D].unsqueeze(1).to_broadcast([P, QT, D]),
                op=mybir.AluOpType.add,
            )

        def late_product(u):
            q, j = divmod(u - LATE, LATE_HEADS)
            if j == 0:
                sums = head_psum.tile([P, QT, D], F32, tag="head")
                head_sum["late", q] = sums
            for g in range(G):
                value_pass(head_sum["late", q][:, j, :], u, g, EARLY_HEADS + j, g)

        def late_add_bias(q):
            nc.vector.tensor_tensor(
                out=o_rows[G_OUT - 1][:, q, K_PASS - LATE_HEADS * D :],
                in0=head_sum["late", q][:, :LATE_HEADS, :].rearrange("p j d -> p (j d)"),
                in1=bias[:, EARLY_HEADS * D :],
                op=mybir.AluOpType.add,
            )

        def turn(c, tiles):
            bank = turn_psum.tile([P, PACK, P], F32, tag="turn")
            turned[c, tiles[0]] = bank
            for n, q in enumerate(tiles):
                words = o_rows[c][:, q, :].bitcast(F32)
                for u in range(2):
                    nc.tensor.transpose(bank[:, 2 * n + u, :], words[:, u : 2 * P : 2], ident[:])

        def first_copy(q):
            dst = o_first[:, q * K_PASS : (q + 2) * K_PASS].bitcast(F32)
            nc.scalar.copy(
                out=dst.rearrange("p (n i u) -> p n i u", n=2, u=2),
                in_=turned[0, q][:].rearrange("p (n u) i -> p n i u", u=2),
            )

        def last_copy(q):
            o_tile = o_pool.tile([P, K_PASS], BF16, align_bytes=64)
            o_last[q] = o_tile
            nc.scalar.copy(
                out=o_tile[:].bitcast(F32).rearrange("p (i u) -> p i u", u=2),
                in_=turned[G_OUT - 1, q][:, :2, :].rearrange("p u i -> p i u"),
            )

        def last_quantise(q):
            o_code = o_pool.tile([P, P], U32, align_bytes=64)
            o_plane = o_pool.tile([P, P], U8, align_bytes=64)
            o_last_code[q] = o_code
            o_last_plane[q] = o_plane
            nc.vector.quantize_mx(out=o_code[:].bitcast(FP8X4), scales=o_plane[:], in_=o_last[q][:])

        def project(q, r, c):
            if c == 0:
                sums = out_psum.tile([P, R_TILE], F32, tag="out")
                out_sum[q, r] = sums
                code, plane = o_first_code[:, q * P : (q + 1) * P], o_first_plane[:, q * P : (q + 1) * P]
            else:
                code, plane = o_last_code[q][:], o_last_plane[q][:]
            nc.tensor.matmul_mx(
                out=out_sum[q, r][:],
                lhsT=code.bitcast(FP8X4),
                lhsT_scale=plane,
                rhs=w_code[c][:, 2 * r * R_TILE : 2 * (r + 1) * R_TILE].bitcast(FP4X4),
                rhs_scale=w_plane[:, c, r * R_TILE : (r + 1) * R_TILE],
                start=(c == 0),
                stop=(c == G_OUT - 1),
            )

        def open_banks(count):
            for n in range(len(out_sum), count):
                project(n // RT, n % RT, 0)

        def store(q, r):
            pair, j = divmod(r, 2)
            if j == 0:
                res = res_pool.tile([P, 2, R_TILE], F32)
                staged[q, pair] = res
            dst = staged[q, pair][:, j, :]
            if q >= QT - 2 and j == 1:
                nc.vector.tensor_copy(out=dst, in_=out_sum[q, r][:])
            else:
                nc.scalar.copy(out=dst, in_=out_sum[q, r][:])
            rows = slice(q * P, (q + 1) * P)
            if q == QT - 1:
                nc.sync.dma_start(out=out[rows, r * R_TILE : (r + 1) * R_TILE], in_=dst)
            elif j == 1:
                nc.sync.dma_start(
                    out=out[rows, (r - 1) * R_TILE : (r + 1) * R_TILE],
                    in_=staged[q, pair][:].rearrange("p j n -> p (j n)"),
                )

        nc.scalar.dma_start(out=first_factor[:], in_=tok_scale[0, :K_PASS].rearrange("(p t) -> p t", t=PACK))
        nc.vector.memset(tok_rows[32:64, :], 0.0)
        nc.vector.memset(tok_rows[64:, :], 0.0)
        nc.scalar.dma_start(out=tok_rows[:CHUNKS, :], in_=tok_scale.rearrange("h (g k) -> (h g) k", g=G))
        nc.scalar.dma_start(out=bias_rows[:], in_=v_bias.rearrange("(p c) -> p c", p=P))
        make_identity(nc, ident[:])
        for plane in v_plane + [w_plane]:
            nc.vector.memset(plane[:].bitcast(U32), 0)
        for k in range(PAIR_BUFS):
            load_pair(k)
        spread_factor()

        product_step = {max(G * (h + 1), FIRST_PRODUCT + LAG * h): h for h in range(EARLY_HEADS)}
        first_done = G * PASS_HEADS + LAG
        head_free = LATE + LAG
        closing = {LATE + LATE_HEADS * (q + 1): q for q in range(QT)}
        last_step = CHUNKS
        held = QT - 2

        scale_chunk(0)
        interleave(0)
        scale_chunk(1)
        scaled, loaded = 2, PAIR_BUFS
        for s in range(last_step + 1):
            if s >= 1:
                quantise(s - 1)
            if s - LAG in product_step:
                early_add_bias(product_step[s - LAG])
            if s == head_free:
                for u in range(LATE, s - 1):
                    late_product(u)
            if s >= head_free:
                late_product(s - 1)
            if s in product_step:
                early_product(product_step[s])
            if s == last_step:
                for r in range(2, RT):
                    project(held, r, 1)
                for r in range(RT - 1):
                    store(held, r)
            if s + 1 < CHUNKS:
                interleave(s + 1)

            if s == FIRST_PRODUCT // 2:
                spread_bias()
            if s == first_done + 1:
                first_copy(0)
            if s in (first_done, first_done + 1):
                turn(0, [2 * (s - first_done), 2 * (s - first_done) + 1])
            if s == first_done + 2:
                first_copy(2)
            if s == first_done + 3:
                nc.vector.quantize_mx(out=o_first_code[:].bitcast(FP8X4), scales=o_first_plane[:], in_=o_first[:])

            if s in closing:
                late_add_bias(closing[s])
                turn(G_OUT - 1, [closing[s]])
            if s - 1 in closing:
                q = closing[s - 1]
                last_quantise(q)
                for r in range(2 if q == held else RT):
                    project(q, r, 1)
            if s + 1 in closing and s + 1 < last_step:
                open_banks(RT * closing[s + 1] + 2)
            if s in closing and s < last_step:
                open_banks(RT * (closing[s] + 1))
            if s - 2 in closing and closing[s - 2] < held:
                for r in range(RT):
                    store(closing[s - 2], r)
            if s in closing:
                last_copy(closing[s])

            while loaded < min(CHUNKS // 2, (s + 2) // 2 + PAIR_BUFS):
                load_pair(loaded)
                loaded = loaded + 1
            while scaled < min(CHUNKS, s + 3 + max(0, (s + 3 - SCALE_AHEAD_FROM) * 3 // 4)):
                scale_chunk(scaled)
                scaled = scaled + 1

        store(held, RT - 1)
        open_banks(QT * RT)
        last_quantise(QT - 1)
        for r in range(RT):
            project(QT - 1, r, 1)
        for r in range(RT):
            store(QT - 1, r)
